import numpy as np
import ml_dtypes


def mxq(x, axis, fmt="e4m3"):
    dtype, down = {"e4m3": (ml_dtypes.float8_e4m3fn, 7), "e5m2": (ml_dtypes.float8_e5m2, 14)}[fmt]
    v = np.moveaxis(np.asarray(x, np.float32).astype(ml_dtypes.bfloat16).astype(np.float64), axis, -1)
    blocks = v.reshape(v.shape[:-1] + (-1, 32))
    amax = np.abs(blocks).max(-1, keepdims=True)
    byte = np.maximum(np.where(amax > 0, np.frexp(amax)[1] - 1 + 127, 0) - down, 1)
    scale = np.exp2(byte - 127.0)
    codes = (blocks / scale).astype(np.float32).astype(dtype).astype(np.float64)
    return np.moveaxis((codes * scale).reshape(v.shape), -1, axis)


WIDE = False


def mx_kscale(k):
    if not WIDE:
        return np.ones(k)
    levels = np.array([10, -10, 5, -5, 0])
    if k % 512:
        return np.exp2(np.random.permutation(np.resize(levels, k // 32))).repeat(32)
    a = np.empty((k // 512, 16))
    for p in range(k // 512):
        a[p, :8] = np.random.permutation(np.resize(levels, 8))
        for g in range(8):
            far = levels[np.abs(levels - a[p, g]) >= 10]
            a[p, g + 8] = far[np.random.randint(len(far))]
    return np.exp2(a.ravel()).repeat(32)


BF16 = ml_dtypes.bfloat16


def bf(x):
    return np.asarray(x, np.float32).astype(BF16)


def f64(x):
    return np.asarray(x).astype(np.float64)


E2M1 = np.array([0.0, 0.5, 1.0, 1.5, 2.0, 3.0, 4.0, 6.0, -0.0, -0.5, -1.0, -1.5, -2.0, -3.0, -4.0, -6.0])


def pack_weight(w, fmt):
    k, n = w.shape
    w = f64(bf(w)).reshape(k // 32, 32, n)
    amax = np.abs(w).max(1)
    if fmt == "e4m3":
        byte = np.frexp(amax)[1] - 1 + 127 - 7
    else:
        mant, ex = np.frexp(amax / 6.0)
        byte = np.where(mant > 0.5, ex, ex - 1) + 127
    byte = np.clip(np.where(amax > 0, byte, 1), 1, 254)
    scaled = (w * np.exp2(127.0 - byte)[:, None, :]).reshape(k, n).astype(np.float32)
    by_word = np.ascontiguousarray(scaled.reshape(k // 512, 128, 4, n).transpose(0, 1, 3, 2))
    if fmt == "e4m3":
        words = by_word.astype(ml_dtypes.float8_e4m3fn).view(np.uint8)
    else:
        c = by_word.astype(ml_dtypes.float4_e2m1fn).view(np.uint8) & 0xF
        words = c[..., 0::2] | (c[..., 1::2] << 4)
    return np.ascontiguousarray(words), np.ascontiguousarray(byte.astype(np.uint8).reshape(k // 512, 16, n))


def unpack_weight(words, scales, fmt):
    g, p, n, _ = words.shape
    if fmt == "e4m3":
        vals = np.ascontiguousarray(words).view(ml_dtypes.float8_e4m3fn).astype(np.float64)
    else:
        nib = np.empty((g, p, n, 4), np.uint8)
        nib[..., 0::2] = words & 0xF
        nib[..., 1::2] = words >> 4
        vals = E2M1[nib]
    vals = vals * np.repeat(np.exp2(scales.astype(np.float64) - 127.0), 8, axis=1)[..., None]
    return vals.transpose(0, 1, 3, 2).reshape(g * 512, n)
def pack4(w):
    words, scales = pack_weight(w, "e2m1")
    return words.reshape(words.shape[0], 128, -1), scales


def unpack4(words, scales):
    return unpack_weight(words.reshape(words.shape[0], 128, -1, 2), scales, "e2m1")


E, S, P = 1024, 2048, 1024


def setup_inputs():
    s, u = mx_kscale(E), mx_kscale(S)
    anomalies = np.random.standard_normal((E, S)) * s[:, None] * u
    transform = np.random.standard_normal((E, E)) / np.sqrt(E) / s[:, None]
    observe = np.random.standard_normal((S, P)) / np.sqrt(S) / u[:, None]
    a_words, a_scales = pack4(anomalies)
    t_words, t_scales = pack4(transform)
    h_words, h_scales = pack_weight(observe, "e4m3")
    return {"a_words": a_words, "a_scales": a_scales,
            "t_words": t_words, "t_scales": t_scales,
            "h_words": h_words, "h_scales": h_scales,
            "infl": bf(1 + 0.1 * np.random.standard_normal(S)),
            "xmean": bf(0.5 * np.random.standard_normal(S) * u),
            "y": bf(np.random.standard_normal(P)),
            "rinv": bf(1 + 0.1 * np.random.standard_normal(P))}


def reference(a_words, a_scales, t_words, t_scales, h_words, h_scales, infl, xmean, y, rinv):
    a = unpack4(a_words, a_scales)
    tr = unpack4(t_words, t_scales)
    h = unpack_weight(h_words, h_scales, "e4m3")
    za = tr.T @ a
    z = za * f64(infl) + f64(xmean)
    obs = mxq(z, 1, "e4m3") @ h
    return (f64(y) - obs) * f64(rinv)

@@ -1,0 +1,247 @@
+from contextlib import ExitStack
+
+import concourse.mybir as mybir
+
+E, S, OBS = 1024, 2048, 1024
+FLOPS = 2 * E * E * S + 2 * E * S * OBS
+
+F32 = mybir.dt.float32
+BF16 = mybir.dt.bfloat16
+I32 = mybir.dt.int32
+U32 = mybir.dt.uint32
+U8 = mybir.dt.uint8
+FP4X4 = mybir.dt.float4_e2m1fn_x4
+FP8X4 = mybir.dt.float8_e4m3fn_x4
+ACT = mybir.ActivationFunctionType
+ALU = mybir.AluOpType
+
+P = 128
+PACK = 4
+KP = P * PACK
+NB = 512
+E_PASSES = E // KP
+S_PASSES = S // KP
+BANKS = 8
+
+STEPS = [(0, 0), (0, 1), (1, 0), (1, 1), (2, 0), (3, 0), (2, 1), (3, 1)]
+
+
+def tile_ensemble_kalman_residual_s4_kernel(
+    tc, a_words, a_scales, t_words, t_scales, h_words, h_scales, infl, xmean, y, rinv, out
+):
+    nc = tc.nc
+    with ExitStack() as ctx:
+        keep = ctx.enter_context(tc.tile_pool(name="keep", bufs=1))
+        work = ctx.enter_context(tc.tile_pool(name="work", bufs=3))
+        psum = ctx.enter_context(tc.psum_pool(name="psum", bufs=1))
+        ctx.enter_context(tc.manual_schedule())
+
+        def kept(name, shape, dtype):
+            return keep.tile(shape, dtype, name=name, align_bytes=64)
+
+        a_raw = [kept("a_raw%d" % sg, [P, E_PASSES, 2 * KP], U8) for sg in range(S_PASSES)]
+        a_cod = [kept("a_cod%d" % sg, [P, E_PASSES, 2 * KP], U8) for sg in range(S_PASSES)]
+        as_raw0 = kept("as_raw0", [P, E_PASSES, KP], U8)
+        as_rawr = kept("as_rawr", [P, E_PASSES, S - KP], U8)
+        a_scl = [kept("a_scl%d" % sg, [P, E_PASSES, KP], U8) for sg in range(S_PASSES)]
+        t_cod = [kept("t_cod%d" % h, [P, E_PASSES, 2 * NB], U8) for h in range(2)]
+        t_scl = kept("t_scl", [P, E_PASSES, E], U8)
+        h_cod = [kept("h_cod%d" % g, [P, OBS], U32) for g in range(S_PASSES)]
+        h_scl = kept("h_scl", [P, OBS], U8)
+        infl_b = kept("infl_b", [P, S_PASSES, PACK], BF16)
+        xmean_b = kept("xmean_b", [P, S_PASSES, PACK], BF16)
+        infl_f = kept("infl_f", [P, S_PASSES, PACK], F32)
+        xmean_f = kept("xmean_f", [P, S_PASSES, PACK], F32)
+        y_b = kept("y_b", [P, OBS], BF16)
+        rinv_b = kept("rinv_b", [P, OBS], BF16)
+        warm = kept("warm", [P, 2], F32)
+        z_pl = [kept("z_pl%d" % i, [P, PACK, NB], BF16) for i in range(len(STEPS))]
+        z_il = [kept("z_il%d" % i, [P, NB, PACK], BF16) for i in range(len(STEPS))]
+        z_cod = [kept("z_cod%d" % i, [P, NB], U32) for i in range(len(STEPS))]
+        z_scl = [kept("z_scl%d" % i, [P, NB], U8) for i in range(len(STEPS))]
+
+        banks_used = []
+
+        def next_bank():
+            b = len(banks_used) % BANKS
+            banks_used.append(b)
+            return psum.tile([P, NB], F32, name="bank%d" % b)
+
+        a_w = a_words.bitcast(I32).rearrange("g p n -> p g n")
+        t_w = t_words.bitcast(I32).rearrange("g p n -> p g n")
+        a_s = a_scales.bitcast(I32).rearrange("g (q r) n -> r q g n", r=4)
+        t_s = t_scales.bitcast(I32).rearrange("g (q r) n -> r q g n", r=4)
+        h_s = h_scales.bitcast(I32)
+
+        def load_a(sg):
+            nc.sync.dma_start(out=a_raw[sg][:].bitcast(I32), in_=a_w[:, :, 256 * sg : 256 * (sg + 1)])
+
+        def load_t(eng, h):
+            eng.dma_start(out=t_cod[h][:].bitcast(I32), in_=t_w[:, :, 256 * h : 256 * (h + 1)])
+
+        def load_scale_rows(eng, plane, src, r):
+            eng.dma_start(out=plane[:].bitcast(I32)[r:P:32, :, :], in_=src)
+
+        nc.vector.memset(as_raw0[:].bitcast(I32), 0)
+        nc.vector.memset(t_scl[:].bitcast(I32), 0)
+        for r in range(4):
+            load_scale_rows(nc.sync, as_raw0, a_s[r][:, :, 0:128], r)
+        nc.scalar.dma_start(out=a_raw[0][:].bitcast(I32), in_=a_w[:, :, 0:256])
+        load_t(nc.scalar, 0)
+        for r in range(4):
+            load_scale_rows(nc.sync, t_scl, t_s[r], r)
+        nc.vector.memset(warm[:], 0.0)
+        nc.vector.memset(as_rawr[:].bitcast(I32), 0)
+        nc.vector.memset(h_scl[:].bitcast(I32), 0)
+        nc.scalar.activation(out=warm[:, 1:2], in_=warm[:, 0:1], func=ACT.Identity, bias=warm[:, 0:1], scale=1.0)
+
+        nc.sync.dma_start(out=infl_b[:], in_=infl.rearrange("(g p t) -> p g t", p=P, t=PACK))
+        nc.sync.dma_start(out=xmean_b[:], in_=xmean.rearrange("(g p t) -> p g t", p=P, t=PACK))
+        load_t(nc.sync, 1)
+        load_a(1)
+        for r in range(4):
+            load_scale_rows(nc.sync, as_rawr, a_s[r][:, :, 128:512], r)
+        load_a(2)
+        load_a(3)
+        for q in range(4):
+            nc.sync.dma_start(out=h_scl[:].bitcast(I32)[32 * q : 32 * q + 16, :], in_=h_s[:, 4 * q : 4 * q + 4, :])
+        for g in range(S_PASSES):
+            nc.sync.dma_start(
+                out=h_cod[g][:].bitcast(I32), in_=h_words[g].rearrange("p n t -> p (n t)").bitcast(I32)
+            )
+        nc.sync.dma_start(out=y_b[:], in_=y.partition_broadcast(P))
+        nc.sync.dma_start(out=rinv_b[:], in_=rinv.partition_broadcast(P))
+
+        nc.scalar.copy(out=infl_f[:], in_=infl_b[:])
+        nc.scalar.copy(out=xmean_f[:], in_=xmean_b[:])
+
+        def raw_scales(sg):
+            return as_raw0[:] if sg == 0 else as_rawr[:, :, KP * (sg - 1) : KP * sg]
+
+        def permute_slot(sg, t):
+            src_s = raw_scales(sg).rearrange("p g (m t) -> p g t m", t=PACK)
+            nc.vector.tensor_copy(out=a_scl[sg][:, :, P * t : P * (t + 1)], in_=src_s[:, :, t, :])
+            src_w = a_raw[sg][:].rearrange("p g (m t b) -> p g t m b", t=PACK, b=2)
+            dst_w = a_cod[sg][:].rearrange("p g (t m b) -> p g t m b", t=PACK, b=2)
+            nc.vector.tensor_copy(out=dst_w[:, :, t, :, :], in_=src_w[:, :, t, :, :])
+
+        def permute(sg):
+            nc.vector.tensor_copy(
+                out=a_scl[sg][:].rearrange("p g (t m) -> p g t m", t=PACK),
+                in_=raw_scales(sg).rearrange("p g (m t) -> p g t m", t=PACK),
+            )
+            for g in range(E_PASSES):
+                nc.vector.tensor_copy(
+                    out=a_cod[sg][:, g, :].rearrange("p (t m b) -> p t m b", t=PACK, b=2),
+                    in_=a_raw[sg][:, g, :].rearrange("p (m t b) -> p t m b", t=PACK, b=2),
+                )
+
+        def stage1(i):
+            sg, h = STEPS[i]
+            for t in range(PACK):
+                bank = next_bank()
+                for g in range(E_PASSES):
+                    nc.tensor.matmul_mx(
+                        out=bank[:],
+                        lhsT=a_cod[sg][:, g, 2 * P * t : 2 * P * (t + 1)].bitcast(FP4X4),
+                        lhsT_scale=a_scl[sg][:, g, P * t : P * (t + 1)],
+                        rhs=t_cod[h][:, g, :].bitcast(FP4X4),
+                        rhs_scale=t_scl[:, g, NB * h : NB * (h + 1)],
+                        start=(g == 0),
+                        stop=(g == E_PASSES - 1),
+                    )
+                nc.scalar.activation(
+                    out=z_pl[i][:, t, :],
+                    in_=bank[:],
+                    func=ACT.Identity,
+                    bias=xmean_f[:, sg, t : t + 1],
+                    scale=infl_f[:, sg, t : t + 1],
+                )
+
+        def interleave(i, on_scalar=False):
+            dst = z_il[i][:].rearrange("p (c j) t -> p c t j", j=4)
+            src = z_pl[i][:].rearrange("p t (c j) -> p c t j", j=4)
+            if on_scalar:
+                nc.scalar.copy(out=dst, in_=src)
+            else:
+                nc.vector.tensor_copy(out=dst, in_=src)
+
+        def quantize(i):
+            nc.vector.quantize_mx(
+                out=z_cod[i][:].bitcast(FP8X4),
+                scales=z_scl[i][:],
+                in_=z_il[i][:].rearrange("p n t -> p (n t)"),
+            )
+
+        for t in range(PACK):
+            permute_slot(0, t)
+        stage1(0)
+        permute(1)
+        stage1(1)
+        interleave(0)
+        stage1(2)
+        permute(2)
+        quantize(0)
+        permute(3)
+        stage1(3)
+        interleave(2)
+        interleave(1)
+        quantize(2)
+        stage1(4)
+        interleave(4)
+        quantize(1)
+        stage1(5)
+        interleave(5)
+        quantize(4)
+        quantize(5)
+        stage1(6)
+        stage1(7)
+        interleave(3)
+        quantize(3)
+        interleave(6, on_scalar=True)
+        interleave(7, on_scalar=True)
+
+        pieces = []
+        for m in range(E // P):
+            widths = [512, 512] if m < E // P - 1 else [512, 256, 128, 128]
+            c0 = 0
+            for w in widths:
+                pieces.append((m, c0, w))
+                c0 += w
+
+        diffs = {}
+
+        def stage2(k):
+            m, c0, w = pieces[k]
+            h, mc = divmod(m * P, NB)
+            bank = next_bank()
+            for g in range(S_PASSES):
+                i = STEPS.index((g, h))
+                nc.tensor.matmul_mx(
+                    out=bank[:, 0:w],
+                    lhsT=z_cod[i][:, mc : mc + P].bitcast(FP8X4),
+                    lhsT_scale=z_scl[i][:, mc : mc + P],
+                    rhs=h_cod[g][:, c0 : c0 + w].bitcast(FP8X4),
+                    rhs_scale=h_scl[4 * g : P, c0 : c0 + w],
+                    start=(g == 0),
+                    stop=(g == S_PASSES - 1),
+                )
+            diff = work.tile([P, NB], F32, name="diff")
+            nc.vector.tensor_tensor(out=diff[:, 0:w], in0=y_b[:, c0 : c0 + w], in1=bank[:, 0:w], op=ALU.subtract)
+            diffs[k] = diff
+
+        def finish(k):
+            m, c0, w = pieces[k]
+            res = work.tile([P, NB], F32, name="res", bufs=6)
+            nc.vector.tensor_tensor(out=res[:, 0:w], in0=diffs[k][:, 0:w], in1=rinv_b[:, c0 : c0 + w], op=ALU.mult)
+            nc.sync.dma_start(out=out[m * P : (m + 1) * P, c0 : c0 + w], in_=res[:, 0:w])
+
+        for k in range(len(pieces)):
+            stage2(k)
+            if k == 3:
+                quantize(6)
+            if k == 5:
+                quantize(7)
+            if k > 0:
+                finish(k - 1)
+        finish(len(pieces) - 1)

@@ -173,6 +173,17 @@ def tile_ensemble_kalman_residual_s4_kernel(
                 in_=z_il[i][:].rearrange("p n t -> p (n t)"),
             )
 
+        idle = next_bank()
+        for rep in range(3):
+            nc.tensor.matmul_mx(
+                out=idle[:],
+                lhsT=a_raw[0][:, 0, 0 : 2 * P].bitcast(FP4X4),
+                lhsT_scale=as_raw0[:, 0, 0:P],
+                rhs=a_raw[0][:, 0, :].bitcast(FP4X4),
+                rhs_scale=as_raw0[:, 0, :],
+                start=True,
+                stop=True,
+            )
         for t in range(PACK):
             permute_slot(0, t)
         stage1(0)
@@ -203,7 +214,7 @@ def tile_ensemble_kalman_residual_s4_kernel(
 
         pieces = []
         for m in range(E // P):
-            widths = [512, 512] if m < E // P - 1 else [512, 256, 128, 128]
+            widths = [512, 512] if m < E // P - 2 else [256, 256, 256, 256]
             c0 = 0
             for w in widths:
                 pieces.append((m, c0, w))
@@ -226,14 +237,18 @@ def tile_ensemble_kalman_residual_s4_kernel(
                     start=(g == 0),
                     stop=(g == S_PASSES - 1),
                 )
-            diff = work.tile([P, NB], F32, name="diff")
+            diff = work.tile([P, NB], F32, name="diff", bufs=4)
             nc.vector.tensor_tensor(out=diff[:, 0:w], in0=y_b[:, c0 : c0 + w], in1=bank[:, 0:w], op=ALU.subtract)
             diffs[k] = diff
+
+        def on_gpsimd(k):
+            return k % 2 == 0 and k < len(pieces) - 3
 
         def finish(k):
             m, c0, w = pieces[k]
             res = work.tile([P, NB], F32, name="res", bufs=6)
-            nc.vector.tensor_tensor(out=res[:, 0:w], in0=diffs[k][:, 0:w], in1=rinv_b[:, c0 : c0 + w], op=ALU.mult)
+            eng = nc.gpsimd if on_gpsimd(k) else nc.vector
+            eng.tensor_tensor(out=res[:, 0:w], in0=diffs[k][:, 0:w], in1=rinv_b[:, c0 : c0 + w], op=ALU.mult)
             nc.sync.dma_start(out=out[m * P : (m + 1) * P, c0 : c0 + w], in_=res[:, 0:w])
 
         for k in range(len(pieces)):
@@ -242,6 +257,8 @@ def tile_ensemble_kalman_residual_s4_kernel(
                 quantize(6)
             if k == 5:
                 quantize(7)
-            if k > 0:
+            if k > 0 and not on_gpsimd(k - 1):
                 finish(k - 1)
+            if on_gpsimd(k):
+                finish(k)
         finish(len(pieces) - 1)

@@ -41,8 +41,8 @@ def tile_ensemble_kalman_residual_s4_kernel(
 
         a_raw = [kept("a_raw%d" % sg, [P, E_PASSES, 2 * KP], U8) for sg in range(S_PASSES)]
         a_cod = [kept("a_cod%d" % sg, [P, E_PASSES, 2 * KP], U8) for sg in range(S_PASSES)]
-        as_raw0 = kept("as_raw0", [P, E_PASSES, KP], U8)
-        as_rawr = kept("as_rawr", [P, E_PASSES, S - KP], U8)
+        as_raw0 = kept("as_raw0", [P, E_PASSES, 2 * KP], U8)
+        as_rawr = kept("as_rawr", [P, E_PASSES, 2 * KP], U8)
         a_scl = [kept("a_scl%d" % sg, [P, E_PASSES, KP], U8) for sg in range(S_PASSES)]
         t_cod = [kept("t_cod%d" % h, [P, E_PASSES, 2 * NB], U8) for h in range(2)]
         t_scl = kept("t_scl", [P, E_PASSES, E], U8)
@@ -85,7 +85,7 @@ def tile_ensemble_kalman_residual_s4_kernel(
         nc.vector.memset(as_raw0[:].bitcast(I32), 0)
         nc.vector.memset(t_scl[:].bitcast(I32), 0)
         for r in range(4):
-            load_scale_rows(nc.sync, as_raw0, a_s[r][:, :, 0:128], r)
+            load_scale_rows(nc.sync, as_raw0, a_s[r][:, :, 0:256], r)
         nc.scalar.dma_start(out=a_raw[0][:].bitcast(I32), in_=a_w[:, :, 0:256])
         load_t(nc.scalar, 0)
         for r in range(4):
@@ -100,7 +100,7 @@ def tile_ensemble_kalman_residual_s4_kernel(
         load_t(nc.sync, 1)
         load_a(1)
         for r in range(4):
-            load_scale_rows(nc.sync, as_rawr, a_s[r][:, :, 128:512], r)
+            load_scale_rows(nc.sync, as_rawr, a_s[r][:, :, 256:512], r)
         load_a(2)
         load_a(3)
         for q in range(4):
@@ -116,7 +116,7 @@ def tile_ensemble_kalman_residual_s4_kernel(
         nc.scalar.copy(out=xmean_f[:], in_=xmean_b[:])
 
         def raw_scales(sg):
-            return as_raw0[:] if sg == 0 else as_rawr[:, :, KP * (sg - 1) : KP * sg]
+            return (as_raw0 if sg < 2 else as_rawr)[:, :, KP * (sg % 2) : KP * (sg % 2 + 1)]
 
         def permute_slot(sg, t):
             src_s = raw_scales(sg).rearrange("p g (m t) -> p g t m", t=PACK)
@@ -126,15 +126,15 @@ def tile_ensemble_kalman_residual_s4_kernel(
             nc.vector.tensor_copy(out=dst_w[:, :, t, :, :], in_=src_w[:, :, t, :, :])
 
         def permute(sg):
-            nc.vector.tensor_copy(
-                out=a_scl[sg][:].rearrange("p g (t m) -> p g t m", t=PACK),
-                in_=raw_scales(sg).rearrange("p g (m t) -> p g t m", t=PACK),
-            )
             for g in range(E_PASSES):
                 nc.vector.tensor_copy(
                     out=a_cod[sg][:, g, :].rearrange("p (t m b) -> p t m b", t=PACK, b=2),
                     in_=a_raw[sg][:, g, :].rearrange("p (m t b) -> p t m b", t=PACK, b=2),
                 )
+            nc.vector.tensor_copy(
+                out=a_scl[sg][:].rearrange("p g (t m) -> p g t m", t=PACK),
+                in_=raw_scales(sg).rearrange("p g (m t) -> p g t m", t=PACK),
+            )
 
         def stage1(i):
             sg, h = STEPS[i]
@@ -180,7 +180,7 @@ def tile_ensemble_kalman_residual_s4_kernel(
                 lhsT=a_raw[0][:, 0, 0 : 2 * P].bitcast(FP4X4),
                 lhsT_scale=as_raw0[:, 0, 0:P],
                 rhs=a_raw[0][:, 0, :].bitcast(FP4X4),
-                rhs_scale=as_raw0[:, 0, :],
+                rhs_scale=as_raw0[:, 0, 0:NB],
                 start=True,
                 stop=True,
             )
@@ -214,7 +214,7 @@ def tile_ensemble_kalman_residual_s4_kernel(
 
         pieces = []
         for m in range(E // P):
-            widths = [512, 512] if m < E // P - 2 else [256, 256, 256, 256]
+            widths = [512, 512] if m < E // P - 1 else [512, 256, 256]
             c0 = 0
             for w in widths:
                 pieces.append((m, c0, w))
@@ -242,7 +242,7 @@ def tile_ensemble_kalman_residual_s4_kernel(
             diffs[k] = diff
 
         def on_gpsimd(k):
-            return k % 2 == 0 and k < len(pieces) - 3
+            return k in (1, 4, 7, 9, 11, 13)
 
         def finish(k):
             m, c0, w = pieces[k]
@@ -255,7 +255,7 @@ def tile_ensemble_kalman_residual_s4_kernel(
             stage2(k)
             if k == 3:
                 quantize(6)
-            if k == 5:
+            if k == 6:
                 quantize(7)
             if k > 0 and not on_gpsimd(k - 1):
                 finish(k - 1)

@@ -9,6 +9,7 @@ F32 = mybir.dt.float32
 BF16 = mybir.dt.bfloat16
 I32 = mybir.dt.int32
 U32 = mybir.dt.uint32
+U16 = mybir.dt.uint16
 U8 = mybir.dt.uint8
 FP4X4 = mybir.dt.float4_e2m1fn_x4
 FP8X4 = mybir.dt.float8_e4m3fn_x4
@@ -21,9 +22,9 @@ KP = P * PACK
 NB = 512
 E_PASSES = E // KP
 S_PASSES = S // KP
+HALVES = E // NB
 BANKS = 8
-
-STEPS = [(0, 0), (0, 1), (1, 0), (1, 1), (2, 0), (3, 0), (2, 1), (3, 1)]
+POOL_COLS = 256
 
 
 def tile_ensemble_kalman_residual_s4_kernel(
@@ -32,7 +33,7 @@ def tile_ensemble_kalman_residual_s4_kernel(
     nc = tc.nc
     with ExitStack() as ctx:
         keep = ctx.enter_context(tc.tile_pool(name="keep", bufs=1))
-        work = ctx.enter_context(tc.tile_pool(name="work", bufs=3))
+        work = ctx.enter_context(tc.tile_pool(name="work", bufs=4))
         psum = ctx.enter_context(tc.psum_pool(name="psum", bufs=1))
         ctx.enter_context(tc.manual_schedule())
 
@@ -40,12 +41,13 @@ def tile_ensemble_kalman_residual_s4_kernel(
             return keep.tile(shape, dtype, name=name, align_bytes=64)
 
         a_raw = [kept("a_raw%d" % sg, [P, E_PASSES, 2 * KP], U8) for sg in range(S_PASSES)]
-        a_cod = [kept("a_cod%d" % sg, [P, E_PASSES, 2 * KP], U8) for sg in range(S_PASSES)]
-        as_raw0 = kept("as_raw0", [P, E_PASSES, 2 * KP], U8)
-        as_rawr = kept("as_rawr", [P, E_PASSES, 2 * KP], U8)
-        a_scl = [kept("a_scl%d" % sg, [P, E_PASSES, KP], U8) for sg in range(S_PASSES)]
-        t_cod = [kept("t_cod%d" % h, [P, E_PASSES, 2 * NB], U8) for h in range(2)]
-        t_scl = kept("t_scl", [P, E_PASSES, E], U8)
+        as_raw = [kept("as_raw%d" % j, [P, E_PASSES, 2 * KP], U8) for j in range(2)]
+        a_cod0 = [kept("a_cod0_%d" % t, [P, E_PASSES, 2 * P], U8) for t in range(PACK)]
+        a_scl0 = [kept("a_scl0_%d" % t, [P, E_PASSES, P], U8) for t in range(PACK)]
+        a_cod = [None] + [kept("a_cod%d" % sg, [P, PACK, E_PASSES, 2 * P], U8) for sg in range(1, S_PASSES)]
+        a_scl = [None] + [kept("a_scl%d" % sg, [P, PACK, E_PASSES, P], U8) for sg in range(1, S_PASSES)]
+        t_cod = [kept("t_cod%d" % h, [P, E_PASSES, 2 * NB], U8) for h in range(HALVES)]
+        t_scl = [kept("t_scl%d" % h, [P, E_PASSES, NB], U8) for h in range(HALVES)]
         h_cod = [kept("h_cod%d" % g, [P, OBS], U32) for g in range(S_PASSES)]
         h_scl = kept("h_scl", [P, OBS], U8)
         infl_b = kept("infl_b", [P, S_PASSES, PACK], BF16)
@@ -54,11 +56,11 @@ def tile_ensemble_kalman_residual_s4_kernel(
         xmean_f = kept("xmean_f", [P, S_PASSES, PACK], F32)
         y_b = kept("y_b", [P, OBS], BF16)
         rinv_b = kept("rinv_b", [P, OBS], BF16)
-        warm = kept("warm", [P, 2], F32)
-        z_pl = [kept("z_pl%d" % i, [P, PACK, NB], BF16) for i in range(len(STEPS))]
-        z_il = [kept("z_il%d" % i, [P, NB, PACK], BF16) for i in range(len(STEPS))]
-        z_cod = [kept("z_cod%d" % i, [P, NB], U32) for i in range(len(STEPS))]
-        z_scl = [kept("z_scl%d" % i, [P, NB], U8) for i in range(len(STEPS))]
+        steps = [(sg, h) for h in range(HALVES) for sg in range(S_PASSES)]
+        z_pl = {s: kept("z_pl%d_%d" % s, [P, PACK, NB], BF16) for s in steps}
+        z_il = {s: kept("z_il%d_%d" % s, [P, NB, PACK], BF16) for s in steps}
+        z_cod = {s: kept("z_cod%d_%d" % s, [P, NB], U32) for s in steps}
+        z_scl = {s: kept("z_scl%d_%d" % s, [P, NB], U8) for s in steps}
 
         banks_used = []
 
@@ -73,36 +75,37 @@ def tile_ensemble_kalman_residual_s4_kernel(
         t_s = t_scales.bitcast(I32).rearrange("g (q r) n -> r q g n", r=4)
         h_s = h_scales.bitcast(I32)
 
-        def load_a(sg):
-            nc.sync.dma_start(out=a_raw[sg][:].bitcast(I32), in_=a_w[:, :, 256 * sg : 256 * (sg + 1)])
+        def load_a(eng, sg):
+            eng.dma_start(out=a_raw[sg][:].bitcast(I32), in_=a_w[:, :, 256 * sg : 256 * (sg + 1)])
 
         def load_t(eng, h):
             eng.dma_start(out=t_cod[h][:].bitcast(I32), in_=t_w[:, :, 256 * h : 256 * (h + 1)])
 
-        def load_scale_rows(eng, plane, src, r):
-            eng.dma_start(out=plane[:].bitcast(I32)[r:P:32, :, :], in_=src)
+        def load_a_scales(j):
+            for r in range(4):
+                nc.sync.dma_start(out=as_raw[j][:].bitcast(I32)[r:P:32], in_=a_s[r][:, :, 256 * j : 256 * (j + 1)])
 
-        nc.vector.memset(as_raw0[:].bitcast(I32), 0)
-        nc.vector.memset(t_scl[:].bitcast(I32), 0)
-        for r in range(4):
-            load_scale_rows(nc.sync, as_raw0, a_s[r][:, :, 0:256], r)
-        nc.scalar.dma_start(out=a_raw[0][:].bitcast(I32), in_=a_w[:, :, 0:256])
+        def load_t_scales(h):
+            for r in range(4):
+                nc.sync.dma_start(out=t_scl[h][:].bitcast(I32)[r:P:32], in_=t_s[r][:, :, 128 * h : 128 * (h + 1)])
+
+        nc.vector.memset(as_raw[0][:].bitcast(I32), 0)
+        nc.vector.memset(t_scl[0][:].bitcast(I32), 0)
+        nc.gpsimd.dma_start(out=infl_b[:], in_=infl.rearrange("(g p t) -> p g t", p=P, t=PACK))
+        nc.gpsimd.dma_start(out=xmean_b[:], in_=xmean.rearrange("(g p t) -> p g t", p=P, t=PACK))
+        load_a_scales(0)
+        load_a(nc.scalar, 0)
         load_t(nc.scalar, 0)
-        for r in range(4):
-            load_scale_rows(nc.sync, t_scl, t_s[r], r)
-        nc.vector.memset(warm[:], 0.0)
-        nc.vector.memset(as_rawr[:].bitcast(I32), 0)
+        load_t_scales(0)
+        nc.vector.memset(as_raw[1][:].bitcast(I32), 0)
+        nc.vector.memset(t_scl[1][:].bitcast(I32), 0)
         nc.vector.memset(h_scl[:].bitcast(I32), 0)
-        nc.scalar.activation(out=warm[:, 1:2], in_=warm[:, 0:1], func=ACT.Identity, bias=warm[:, 0:1], scale=1.0)
-
-        nc.sync.dma_start(out=infl_b[:], in_=infl.rearrange("(g p t) -> p g t", p=P, t=PACK))
-        nc.sync.dma_start(out=xmean_b[:], in_=xmean.rearrange("(g p t) -> p g t", p=P, t=PACK))
+        load_a(nc.sync, 1)
+        load_a_scales(1)
+        load_a(nc.sync, 2)
+        load_a(nc.sync, 3)
+        load_t_scales(1)
         load_t(nc.sync, 1)
-        load_a(1)
-        for r in range(4):
-            load_scale_rows(nc.sync, as_rawr, a_s[r][:, :, 256:512], r)
-        load_a(2)
-        load_a(3)
         for q in range(4):
             nc.sync.dma_start(out=h_scl[:].bitcast(I32)[32 * q : 32 * q + 16, :], in_=h_s[:, 4 * q : 4 * q + 4, :])
         for g in range(S_PASSES):
@@ -112,153 +115,152 @@ def tile_ensemble_kalman_residual_s4_kernel(
         nc.sync.dma_start(out=y_b[:], in_=y.partition_broadcast(P))
         nc.sync.dma_start(out=rinv_b[:], in_=rinv.partition_broadcast(P))
 
-        nc.scalar.copy(out=infl_f[:], in_=infl_b[:])
-        nc.scalar.copy(out=xmean_f[:], in_=xmean_b[:])
+        nc.scalar.activation(out=infl_f[:], in_=infl_b[:], func=ACT.Identity)
+        nc.scalar.activation(out=xmean_f[:], in_=xmean_b[:], func=ACT.Identity)
 
         def raw_scales(sg):
-            return (as_raw0 if sg < 2 else as_rawr)[:, :, KP * (sg % 2) : KP * (sg % 2 + 1)]
+            return as_raw[sg // 2][:, :, KP * (sg % 2) : KP * (sg % 2 + 1)].rearrange("p g (m t) -> p t g m", t=PACK)
 
-        def permute_slot(sg, t):
-            src_s = raw_scales(sg).rearrange("p g (m t) -> p g t m", t=PACK)
-            nc.vector.tensor_copy(out=a_scl[sg][:, :, P * t : P * (t + 1)], in_=src_s[:, :, t, :])
-            src_w = a_raw[sg][:].rearrange("p g (m t b) -> p g t m b", t=PACK, b=2)
-            dst_w = a_cod[sg][:].rearrange("p g (t m b) -> p g t m b", t=PACK, b=2)
-            nc.vector.tensor_copy(out=dst_w[:, :, t, :, :], in_=src_w[:, :, t, :, :])
+        def raw_words(sg):
+            return a_raw[sg][:].bitcast(U16).rearrange("p g (m t) -> p t g m", t=PACK)
 
-        def permute(sg):
-            for g in range(E_PASSES):
-                nc.vector.tensor_copy(
-                    out=a_cod[sg][:, g, :].rearrange("p (t m b) -> p t m b", t=PACK, b=2),
-                    in_=a_raw[sg][:, g, :].rearrange("p (m t b) -> p t m b", t=PACK, b=2),
-                )
-            nc.vector.tensor_copy(
-                out=a_scl[sg][:].rearrange("p g (t m) -> p g t m", t=PACK),
-                in_=raw_scales(sg).rearrange("p g (m t) -> p g t m", t=PACK),
-            )
+        def deal_slot(t):
+            nc.vector.tensor_copy(out=a_cod0[t][:].bitcast(U16), in_=raw_words(0)[:, t])
+            nc.vector.tensor_copy(out=a_scl0[t][:], in_=raw_scales(0)[:, t])
 
-        def stage1(i):
-            sg, h = STEPS[i]
+        def deal(sg):
+            nc.vector.tensor_copy(out=a_cod[sg][:].bitcast(U16), in_=raw_words(sg))
+            nc.vector.tensor_copy(out=a_scl[sg][:], in_=raw_scales(sg))
+
+        def stage1(sg, h):
             for t in range(PACK):
+                cod = a_cod0[t][:] if sg == 0 else a_cod[sg][:, t]
+                scl = a_scl0[t][:] if sg == 0 else a_scl[sg][:, t]
                 bank = next_bank()
                 for g in range(E_PASSES):
                     nc.tensor.matmul_mx(
                         out=bank[:],
-                        lhsT=a_cod[sg][:, g, 2 * P * t : 2 * P * (t + 1)].bitcast(FP4X4),
-                        lhsT_scale=a_scl[sg][:, g, P * t : P * (t + 1)],
+                        lhsT=cod[:, g, :].bitcast(FP4X4),
+                        lhsT_scale=scl[:, g, :],
                         rhs=t_cod[h][:, g, :].bitcast(FP4X4),
-                        rhs_scale=t_scl[:, g, NB * h : NB * (h + 1)],
+                        rhs_scale=t_scl[h][:, g, :],
                         start=(g == 0),
                         stop=(g == E_PASSES - 1),
                     )
                 nc.scalar.activation(
-                    out=z_pl[i][:, t, :],
+                    out=z_pl[sg, h][:, t, :],
                     in_=bank[:],
                     func=ACT.Identity,
                     bias=xmean_f[:, sg, t : t + 1],
                     scale=infl_f[:, sg, t : t + 1],
                 )
 
-        def interleave(i, on_scalar=False):
-            dst = z_il[i][:].rearrange("p (c j) t -> p c t j", j=4)
-            src = z_pl[i][:].rearrange("p t (c j) -> p c t j", j=4)
+        def interleave(sg, h, on_scalar=False):
+            dst = z_il[sg, h][:].rearrange("p (c j) t -> p c t j", j=4)
+            src = z_pl[sg, h][:].rearrange("p t (c j) -> p c t j", j=4)
             if on_scalar:
                 nc.scalar.copy(out=dst, in_=src)
             else:
                 nc.vector.tensor_copy(out=dst, in_=src)
 
-        def quantize(i):
+        def quantize(sg, h):
             nc.vector.quantize_mx(
-                out=z_cod[i][:].bitcast(FP8X4),
-                scales=z_scl[i][:],
-                in_=z_il[i][:].rearrange("p n t -> p (n t)"),
+                out=z_cod[sg, h][:].bitcast(FP8X4),
+                scales=z_scl[sg, h][:],
+                in_=z_il[sg, h][:].rearrange("p n t -> p (n t)"),
             )
-
-        idle = next_bank()
-        for rep in range(3):
-            nc.tensor.matmul_mx(
-                out=idle[:],
-                lhsT=a_raw[0][:, 0, 0 : 2 * P].bitcast(FP4X4),
-                lhsT_scale=as_raw0[:, 0, 0:P],
-                rhs=a_raw[0][:, 0, :].bitcast(FP4X4),
-                rhs_scale=as_raw0[:, 0, 0:NB],
-                start=True,
-                stop=True,
-            )
-        for t in range(PACK):
-            permute_slot(0, t)
-        stage1(0)
-        permute(1)
-        stage1(1)
-        interleave(0)
-        stage1(2)
-        permute(2)
-        quantize(0)
-        permute(3)
-        stage1(3)
-        interleave(2)
-        interleave(1)
-        quantize(2)
-        stage1(4)
-        interleave(4)
-        quantize(1)
-        stage1(5)
-        interleave(5)
-        quantize(4)
-        quantize(5)
-        stage1(6)
-        stage1(7)
-        interleave(3)
-        quantize(3)
-        interleave(6, on_scalar=True)
-        interleave(7, on_scalar=True)
 
         pieces = []
         for m in range(E // P):
-            widths = [512, 512] if m < E // P - 1 else [512, 256, 256]
+            widths = [512, 512] if m < E // P - 1 else [256, 256, 256, 128, 128]
             c0 = 0
             for w in widths:
                 pieces.append((m, c0, w))
                 c0 += w
+        first_narrow = len(pieces) - 5
 
         diffs = {}
+        results = {}
+
+        def pool_columns(k):
+            m, c0, w = pieces[k]
+            if w == NB:
+                return POOL_COLS
+            return w if k == first_narrow + 1 else 0
 
         def stage2(k):
             m, c0, w = pieces[k]
             h, mc = divmod(m * P, NB)
             bank = next_bank()
             for g in range(S_PASSES):
-                i = STEPS.index((g, h))
                 nc.tensor.matmul_mx(
                     out=bank[:, 0:w],
-                    lhsT=z_cod[i][:, mc : mc + P].bitcast(FP8X4),
-                    lhsT_scale=z_scl[i][:, mc : mc + P],
+                    lhsT=z_cod[g, h][:, mc : mc + P].bitcast(FP8X4),
+                    lhsT_scale=z_scl[g, h][:, mc : mc + P],
                     rhs=h_cod[g][:, c0 : c0 + w].bitcast(FP8X4),
                     rhs_scale=h_scl[4 * g : P, c0 : c0 + w],
                     start=(g == 0),
                     stop=(g == S_PASSES - 1),
                 )
-            diff = work.tile([P, NB], F32, name="diff", bufs=4)
-            nc.vector.tensor_tensor(out=diff[:, 0:w], in0=y_b[:, c0 : c0 + w], in1=bank[:, 0:w], op=ALU.subtract)
-            diffs[k] = diff
-
-        def on_gpsimd(k):
-            return k in (1, 4, 7, 9, 11, 13)
+            diffs[k] = work.tile([P, NB], F32, name="diff", bufs=4)
+            results[k] = work.tile([P, NB], F32, name="res", bufs=6)
+            cut = w - pool_columns(k)
+            for lo, hi in ((0, cut), (cut, w)):
+                if hi > lo:
+                    nc.vector.tensor_tensor(
+                        out=diffs[k][:, lo:hi], in0=y_b[:, c0 + lo : c0 + hi], in1=bank[:, lo:hi], op=ALU.subtract
+                    )
 
         def finish(k):
             m, c0, w = pieces[k]
-            res = work.tile([P, NB], F32, name="res", bufs=6)
-            eng = nc.gpsimd if on_gpsimd(k) else nc.vector
-            eng.tensor_tensor(out=res[:, 0:w], in0=diffs[k][:, 0:w], in1=rinv_b[:, c0 : c0 + w], op=ALU.mult)
-            nc.sync.dma_start(out=out[m * P : (m + 1) * P, c0 : c0 + w], in_=res[:, 0:w])
+            cut = w - pool_columns(k)
+            for eng, lo, hi in ((nc.vector, 0, cut), (nc.gpsimd, cut, w)):
+                if hi > lo:
+                    eng.tensor_tensor(
+                        out=results[k][:, lo:hi],
+                        in0=diffs[k][:, lo:hi],
+                        in1=rinv_b[:, c0 + lo : c0 + hi],
+                        op=ALU.mult,
+                    )
+            eng = nc.scalar if k > first_narrow and (len(pieces) - k) % 2 == 1 else nc.sync
+            eng.dma_start(out=out[m * P : (m + 1) * P, c0 : c0 + w], in_=results[k][:, 0:w])
 
-        for k in range(len(pieces)):
+        for t in range(PACK):
+            deal_slot(t)
+        stage1(0, 0)
+        deal(1)
+        stage1(1, 0)
+        deal(2)
+        interleave(0, 0)
+        deal(3)
+        quantize(0, 0)
+        for sg in range(2, S_PASSES):
+            stage1(sg, 0)
+        for sg in range(1, S_PASSES):
+            interleave(sg, 0)
+            quantize(sg, 0)
+        for sg in range(2):
+            stage1(sg, 1)
+            interleave(sg, 1)
+            quantize(sg, 1)
+        stage2(0)
+        finish(0)
+        stage1(2, 1)
+        interleave(2, 1)
+        stage2(1)
+        quantize(2, 1)
+        finish(1)
+        stage1(3, 1)
+        interleave(3, 1, on_scalar=True)
+        for k in range(2, first_narrow):
             stage2(k)
-            if k == 3:
-                quantize(6)
-            if k == 6:
-                quantize(7)
-            if k > 0 and not on_gpsimd(k - 1):
+            finish(k)
+            if k == 5:
+                quantize(3, 1)
+        for k in range(first_narrow, len(pieces)):
+            stage2(k)
+            if k > first_narrow and pool_columns(k - 1) == 0:
                 finish(k - 1)
-            if on_gpsimd(k):
+            if pool_columns(k) > 0:
                 finish(k)
         finish(len(pieces) - 1)

@@ -225,6 +225,17 @@ def tile_ensemble_kalman_residual_s4_kernel(
             eng = nc.scalar if k > first_narrow and (len(pieces) - k) % 2 == 1 else nc.sync
             eng.dma_start(out=out[m * P : (m + 1) * P, c0 : c0 + w], in_=results[k][:, 0:w])
 
+        idle = next_bank()
+        for rep in range(3):
+            nc.tensor.matmul_mx(
+                out=idle[:],
+                lhsT=as_raw[0][:, 0, 0 : 2 * P].bitcast(FP4X4),
+                lhsT_scale=as_raw[0][:, 0, 0:P],
+                rhs=as_raw[0][:, 0, :].bitcast(FP4X4),
+                rhs_scale=as_raw[0][:, 0, 0:NB],
+                start=True,
+                stop=True,
+            )
         for t in range(PACK):
             deal_slot(t)
         stage1(0, 0)

@@ -24,7 +24,6 @@ E_PASSES = E // KP
 S_PASSES = S // KP
 HALVES = E // NB
 BANKS = 8
-POOL_COLS = 256
 
 
 def tile_ensemble_kalman_residual_s4_kernel(
@@ -47,7 +46,7 @@ def tile_ensemble_kalman_residual_s4_kernel(
         a_cod = [None] + [kept("a_cod%d" % sg, [P, PACK, E_PASSES, 2 * P], U8) for sg in range(1, S_PASSES)]
         a_scl = [None] + [kept("a_scl%d" % sg, [P, PACK, E_PASSES, P], U8) for sg in range(1, S_PASSES)]
         t_cod = [kept("t_cod%d" % h, [P, E_PASSES, 2 * NB], U8) for h in range(HALVES)]
-        t_scl = [kept("t_scl%d" % h, [P, E_PASSES, NB], U8) for h in range(HALVES)]
+        t_scl = kept("t_scl", [P, E_PASSES, E], U8)
         h_cod = [kept("h_cod%d" % g, [P, OBS], U32) for g in range(S_PASSES)]
         h_scl = kept("h_scl", [P, OBS], U8)
         infl_b = kept("infl_b", [P, S_PASSES, PACK], BF16)
@@ -85,27 +84,25 @@ def tile_ensemble_kalman_residual_s4_kernel(
             for r in range(4):
                 nc.sync.dma_start(out=as_raw[j][:].bitcast(I32)[r:P:32], in_=a_s[r][:, :, 256 * j : 256 * (j + 1)])
 
-        def load_t_scales(h):
+        def load_t_scales():
             for r in range(4):
-                nc.sync.dma_start(out=t_scl[h][:].bitcast(I32)[r:P:32], in_=t_s[r][:, :, 128 * h : 128 * (h + 1)])
+                nc.sync.dma_start(out=t_scl[:].bitcast(I32)[r:P:32], in_=t_s[r])
 
         nc.vector.memset(as_raw[0][:].bitcast(I32), 0)
-        nc.vector.memset(t_scl[0][:].bitcast(I32), 0)
-        nc.gpsimd.dma_start(out=infl_b[:], in_=infl.rearrange("(g p t) -> p g t", p=P, t=PACK))
-        nc.gpsimd.dma_start(out=xmean_b[:], in_=xmean.rearrange("(g p t) -> p g t", p=P, t=PACK))
+        nc.vector.memset(t_scl[:].bitcast(I32), 0)
         load_a_scales(0)
         load_a(nc.scalar, 0)
         load_t(nc.scalar, 0)
-        load_t_scales(0)
+        load_t_scales()
+        nc.sync.dma_start(out=infl_b[:], in_=infl.rearrange("(g p t) -> p g t", p=P, t=PACK))
+        nc.sync.dma_start(out=xmean_b[:], in_=xmean.rearrange("(g p t) -> p g t", p=P, t=PACK))
         nc.vector.memset(as_raw[1][:].bitcast(I32), 0)
-        nc.vector.memset(t_scl[1][:].bitcast(I32), 0)
         nc.vector.memset(h_scl[:].bitcast(I32), 0)
+        load_t(nc.sync, 1)
         load_a(nc.sync, 1)
         load_a_scales(1)
         load_a(nc.sync, 2)
         load_a(nc.sync, 3)
-        load_t_scales(1)
-        load_t(nc.sync, 1)
         for q in range(4):
             nc.sync.dma_start(out=h_scl[:].bitcast(I32)[32 * q : 32 * q + 16, :], in_=h_s[:, 4 * q : 4 * q + 4, :])
         for g in range(S_PASSES):
@@ -143,7 +140,7 @@ def tile_ensemble_kalman_residual_s4_kernel(
                         lhsT=cod[:, g, :].bitcast(FP4X4),
                         lhsT_scale=scl[:, g, :],
                         rhs=t_cod[h][:, g, :].bitcast(FP4X4),
-                        rhs_scale=t_scl[h][:, g, :],
+                        rhs_scale=t_scl[:, g, NB * h : NB * (h + 1)],
                         start=(g == 0),
                         stop=(g == E_PASSES - 1),
                     )
@@ -172,21 +169,19 @@ def tile_ensemble_kalman_residual_s4_kernel(
 
         pieces = []
         for m in range(E // P):
-            widths = [512, 512] if m < E // P - 1 else [256, 256, 256, 128, 128]
+            widths = [512, 512] if m < E // P - 1 else [512, 256, 256]
             c0 = 0
             for w in widths:
                 pieces.append((m, c0, w))
                 c0 += w
-        first_narrow = len(pieces) - 5
+        first_narrow = len(pieces) - 3
 
         diffs = {}
         results = {}
 
         def pool_columns(k):
             m, c0, w = pieces[k]
-            if w == NB:
-                return POOL_COLS
-            return w if k == first_narrow + 1 else 0
+            return w if k % 2 == 1 and k < first_narrow else 0
 
         def stage2(k):
             m, c0, w = pieces[k]
@@ -204,24 +199,19 @@ def tile_ensemble_kalman_residual_s4_kernel(
                 )
             diffs[k] = work.tile([P, NB], F32, name="diff", bufs=4)
             results[k] = work.tile([P, NB], F32, name="res", bufs=6)
-            cut = w - pool_columns(k)
-            for lo, hi in ((0, cut), (cut, w)):
-                if hi > lo:
-                    nc.vector.tensor_tensor(
-                        out=diffs[k][:, lo:hi], in0=y_b[:, c0 + lo : c0 + hi], in1=bank[:, lo:hi], op=ALU.subtract
-                    )
+            nc.vector.tensor_tensor(out=diffs[k][:, 0:w], in0=y_b[:, c0 : c0 + w], in1=bank[:, 0:w], op=ALU.subtract)
+            multiply(k, nc.gpsimd, w - pool_columns(k), w)
+
+        def multiply(k, eng, lo, hi):
+            m, c0, w = pieces[k]
+            if hi > lo:
+                eng.tensor_tensor(
+                    out=results[k][:, lo:hi], in0=diffs[k][:, lo:hi], in1=rinv_b[:, c0 + lo : c0 + hi], op=ALU.mult
+                )
 
         def finish(k):
             m, c0, w = pieces[k]
-            cut = w - pool_columns(k)
-            for eng, lo, hi in ((nc.vector, 0, cut), (nc.gpsimd, cut, w)):
-                if hi > lo:
-                    eng.tensor_tensor(
-                        out=results[k][:, lo:hi],
-                        in0=diffs[k][:, lo:hi],
-                        in1=rinv_b[:, c0 + lo : c0 + hi],
-                        op=ALU.mult,
-                    )
+            multiply(k, nc.vector, 0, w - pool_columns(k))
             eng = nc.scalar if k > first_narrow and (len(pieces) - k) % 2 == 1 else nc.sync
             eng.dma_start(out=out[m * P : (m + 1) * P, c0 : c0 + w], in_=results[k][:, 0:w])
 
@@ -240,38 +230,23 @@ def tile_ensemble_kalman_residual_s4_kernel(
             deal_slot(t)
         stage1(0, 0)
         deal(1)
-        stage1(1, 0)
+        stage1(0, 1)
         deal(2)
         interleave(0, 0)
         deal(3)
         quantize(0, 0)
-        for sg in range(2, S_PASSES):
-            stage1(sg, 0)
-        for sg in range(1, S_PASSES):
-            interleave(sg, 0)
-            quantize(sg, 0)
-        for sg in range(2):
-            stage1(sg, 1)
-            interleave(sg, 1)
-            quantize(sg, 1)
-        stage2(0)
-        finish(0)
-        stage1(2, 1)
-        interleave(2, 1)
-        stage2(1)
-        quantize(2, 1)
-        finish(1)
+        interleave(0, 1)
+        quantize(0, 1)
+        for sg, h in [(1, 0), (2, 0), (3, 0), (1, 1), (2, 1)]:
+            stage1(sg, h)
+            interleave(sg, h)
+            quantize(sg, h)
         stage1(3, 1)
         interleave(3, 1, on_scalar=True)
-        for k in range(2, first_narrow):
+        for k in range(len(pieces)):
             stage2(k)
-            finish(k)
-            if k == 5:
-                quantize(3, 1)
-        for k in range(first_narrow, len(pieces)):
-            stage2(k)
-            if k > first_narrow and pool_columns(k - 1) == 0:
+            if k > 0:
                 finish(k - 1)
-            if pool_columns(k) > 0:
-                finish(k)
+            if k == 3:
+                quantize(3, 1)
         finish(len(pieces) - 1)

@@ -40,7 +40,8 @@ def tile_ensemble_kalman_residual_s4_kernel(
             return keep.tile(shape, dtype, name=name, align_bytes=64)
 
         a_raw = [kept("a_raw%d" % sg, [P, E_PASSES, 2 * KP], U8) for sg in range(S_PASSES)]
-        as_raw = [kept("as_raw%d" % j, [P, E_PASSES, 2 * KP], U8) for j in range(2)]
+        as_first = kept("as_first", [P, E_PASSES, KP], U8)
+        as_rest = kept("as_rest", [P, E_PASSES, S - KP], U8)
         a_cod0 = [kept("a_cod0_%d" % t, [P, E_PASSES, 2 * P], U8) for t in range(PACK)]
         a_scl0 = [kept("a_scl0_%d" % t, [P, E_PASSES, P], U8) for t in range(PACK)]
         a_cod = [None] + [kept("a_cod%d" % sg, [P, PACK, E_PASSES, 2 * P], U8) for sg in range(1, S_PASSES)]
@@ -80,27 +81,23 @@ def tile_ensemble_kalman_residual_s4_kernel(
         def load_t(eng, h):
             eng.dma_start(out=t_cod[h][:].bitcast(I32), in_=t_w[:, :, 256 * h : 256 * (h + 1)])
 
-        def load_a_scales(j):
+        def load_scale_rows(plane, rows, queues):
             for r in range(4):
-                nc.sync.dma_start(out=as_raw[j][:].bitcast(I32)[r:P:32], in_=a_s[r][:, :, 256 * j : 256 * (j + 1)])
+                queues[r].dma_start(out=plane[:].bitcast(I32)[r:P:32], in_=rows[r])
 
-        def load_t_scales():
-            for r in range(4):
-                nc.sync.dma_start(out=t_scl[:].bitcast(I32)[r:P:32], in_=t_s[r])
-
-        nc.vector.memset(as_raw[0][:].bitcast(I32), 0)
+        nc.vector.memset(as_first[:].bitcast(I32), 0)
         nc.vector.memset(t_scl[:].bitcast(I32), 0)
-        load_a_scales(0)
+        load_scale_rows(as_first, a_s[:, :, :, 0:128], [nc.sync, nc.scalar, nc.sync, nc.sync])
         load_a(nc.scalar, 0)
         load_t(nc.scalar, 0)
-        load_t_scales()
+        load_scale_rows(t_scl, t_s, [nc.sync, nc.sync, nc.sync, nc.scalar])
         nc.sync.dma_start(out=infl_b[:], in_=infl.rearrange("(g p t) -> p g t", p=P, t=PACK))
         nc.sync.dma_start(out=xmean_b[:], in_=xmean.rearrange("(g p t) -> p g t", p=P, t=PACK))
-        nc.vector.memset(as_raw[1][:].bitcast(I32), 0)
+        nc.vector.memset(as_rest[:].bitcast(I32), 0)
         nc.vector.memset(h_scl[:].bitcast(I32), 0)
         load_t(nc.sync, 1)
         load_a(nc.sync, 1)
-        load_a_scales(1)
+        load_scale_rows(as_rest, a_s[:, :, :, 128:512], [nc.sync] * 4)
         load_a(nc.sync, 2)
         load_a(nc.sync, 3)
         for q in range(4):
@@ -116,7 +113,8 @@ def tile_ensemble_kalman_residual_s4_kernel(
         nc.scalar.activation(out=xmean_f[:], in_=xmean_b[:], func=ACT.Identity)
 
         def raw_scales(sg):
-            return as_raw[sg // 2][:, :, KP * (sg % 2) : KP * (sg % 2 + 1)].rearrange("p g (m t) -> p t g m", t=PACK)
+            raw = as_first[:] if sg == 0 else as_rest[:, :, KP * (sg - 1) : KP * sg]
+            return raw.rearrange("p g (m t) -> p t g m", t=PACK)
 
         def raw_words(sg):
             return a_raw[sg][:].bitcast(U16).rearrange("p g (m t) -> p t g m", t=PACK)
@@ -216,13 +214,13 @@ def tile_ensemble_kalman_residual_s4_kernel(
             eng.dma_start(out=out[m * P : (m + 1) * P, c0 : c0 + w], in_=results[k][:, 0:w])
 
         idle = next_bank()
-        for rep in range(3):
+        for rep in range(2):
             nc.tensor.matmul_mx(
                 out=idle[:],
-                lhsT=as_raw[0][:, 0, 0 : 2 * P].bitcast(FP4X4),
-                lhsT_scale=as_raw[0][:, 0, 0:P],
-                rhs=as_raw[0][:, 0, :].bitcast(FP4X4),
-                rhs_scale=as_raw[0][:, 0, 0:NB],
+                lhsT=as_first[:, 0, 0 : 2 * P].bitcast(FP4X4),
+                lhsT_scale=as_first[:, 0, 0:P],
+                rhs=as_first[:].rearrange("p g n -> p (g n)").bitcast(FP4X4),
+                rhs_scale=as_first[:, 0, :],
                 start=True,
                 stop=True,
             )

@@ -1,3 +1,4 @@
+import math
 from contextlib import ExitStack
 
 import concourse.mybir as mybir
@@ -24,6 +25,9 @@ E_PASSES = E // KP
 S_PASSES = S // KP
 HALVES = E // NB
 BANKS = 8
+WIDTH = {F32: 4, U32: 4, BF16: 2, U8: 1}
+SPAN = 256
+STATIONARY_SHIFT = 64
 
 
 def tile_ensemble_kalman_residual_s4_kernel(
@@ -36,16 +40,20 @@ def tile_ensemble_kalman_residual_s4_kernel(
         psum = ctx.enter_context(tc.psum_pool(name="psum", bufs=1))
         ctx.enter_context(tc.manual_schedule())
 
-        def kept(name, shape, dtype):
-            return keep.tile(shape, dtype, name=name, align_bytes=64)
+        ends = [0]
+
+        def kept(name, shape, dtype, shift=0):
+            start = (ends[-1] + SPAN - 1) // SPAN * SPAN + shift
+            ends.append(start + math.prod(shape[1:]) * WIDTH[dtype])
+            return keep.tile(shape, dtype, name=name, align_bytes=SPAN if start == 0 else 64, offset=start)
 
         a_raw = [kept("a_raw%d" % sg, [P, E_PASSES, 2 * KP], U8) for sg in range(S_PASSES)]
         as_first = kept("as_first", [P, E_PASSES, KP], U8)
         as_rest = kept("as_rest", [P, E_PASSES, S - KP], U8)
-        a_cod0 = [kept("a_cod0_%d" % t, [P, E_PASSES, 2 * P], U8) for t in range(PACK)]
-        a_scl0 = [kept("a_scl0_%d" % t, [P, E_PASSES, P], U8) for t in range(PACK)]
-        a_cod = [None] + [kept("a_cod%d" % sg, [P, PACK, E_PASSES, 2 * P], U8) for sg in range(1, S_PASSES)]
-        a_scl = [None] + [kept("a_scl%d" % sg, [P, PACK, E_PASSES, P], U8) for sg in range(1, S_PASSES)]
+        a_cod0 = [kept("a_cod0_%d" % t, [P, E_PASSES, 2 * P], U8, STATIONARY_SHIFT) for t in range(PACK)]
+        a_scl0 = [kept("a_scl0_%d" % t, [P, E_PASSES, P], U8, STATIONARY_SHIFT) for t in range(PACK)]
+        a_cod = [None] + [kept("a_cod%d" % sg, [P, PACK, E_PASSES, 2 * P], U8, STATIONARY_SHIFT) for sg in range(1, S_PASSES)]
+        a_scl = [None] + [kept("a_scl%d" % sg, [P, PACK, E_PASSES, P], U8, STATIONARY_SHIFT) for sg in range(1, S_PASSES)]
         t_cod = [kept("t_cod%d" % h, [P, E_PASSES, 2 * NB], U8) for h in range(HALVES)]
         t_scl = kept("t_scl", [P, E_PASSES, E], U8)
         h_cod = [kept("h_cod%d" % g, [P, OBS], U32) for g in range(S_PASSES)]
@@ -59,8 +67,8 @@ def tile_ensemble_kalman_residual_s4_kernel(
         steps = [(sg, h) for h in range(HALVES) for sg in range(S_PASSES)]
         z_pl = {s: kept("z_pl%d_%d" % s, [P, PACK, NB], BF16) for s in steps}
         z_il = {s: kept("z_il%d_%d" % s, [P, NB, PACK], BF16) for s in steps}
-        z_cod = {s: kept("z_cod%d_%d" % s, [P, NB], U32) for s in steps}
-        z_scl = {s: kept("z_scl%d_%d" % s, [P, NB], U8) for s in steps}
+        z_cod = {s: kept("z_cod%d_%d" % s, [P, NB], U32, STATIONARY_SHIFT) for s in steps}
+        z_scl = {s: kept("z_scl%d_%d" % s, [P, NB], U8, STATIONARY_SHIFT) for s in steps}
 
         banks_used = []
 

@@ -242,17 +242,23 @@ def tile_ensemble_kalman_residual_s4_kernel(
         deal(3)
         quantize(0, 0)
         interleave(0, 1)
-        quantize(0, 1)
-        for sg, h in [(1, 0), (2, 0), (3, 0), (1, 1), (2, 1)]:
-            stage1(sg, h)
-            interleave(sg, h)
-            quantize(sg, h)
+        for before, step in [((0, 1), (1, 0)), ((1, 0), (2, 0)), ((2, 0), (3, 0))]:
+            stage1(*step)
+            interleave(*step)
+            quantize(*before)
+        quantize(3, 0)
+        stage1(1, 1)
+        interleave(1, 1)
+        quantize(1, 1)
+        stage1(2, 1)
+        interleave(2, 1)
         stage1(3, 1)
         interleave(3, 1, on_scalar=True)
+        late = {0: 2, 5: 3}
         for k in range(len(pieces)):
             stage2(k)
             if k > 0:
                 finish(k - 1)
-            if k == 3:
-                quantize(3, 1)
+            if k in late:
+                quantize(late[k], 1)
         finish(len(pieces) - 1)

@@ -89,16 +89,16 @@ def tile_ensemble_kalman_residual_s4_kernel(
         def load_t(eng, h):
             eng.dma_start(out=t_cod[h][:].bitcast(I32), in_=t_w[:, :, 256 * h : 256 * (h + 1)])
 
-        def load_scale_rows(plane, rows, queues):
-            for r in range(4):
+        def load_scale_rows(plane, rows, queues, which=range(4)):
+            for r in which:
                 queues[r].dma_start(out=plane[:].bitcast(I32)[r:P:32], in_=rows[r])
 
         nc.vector.memset(as_first[:].bitcast(I32), 0)
         nc.vector.memset(t_scl[:].bitcast(I32), 0)
-        load_scale_rows(as_first, a_s[:, :, :, 0:128], [nc.sync, nc.scalar, nc.sync, nc.sync])
-        load_a(nc.scalar, 0)
+        load_scale_rows(as_first, a_s[:, :, :, 0:128], [nc.sync, nc.scalar] * 2)
+        load_a(nc.sync, 0)
         load_t(nc.scalar, 0)
-        load_scale_rows(t_scl, t_s, [nc.sync, nc.sync, nc.sync, nc.scalar])
+        load_scale_rows(t_scl, t_s, [nc.sync, nc.scalar] * 2)
         nc.sync.dma_start(out=infl_b[:], in_=infl.rearrange("(g p t) -> p g t", p=P, t=PACK))
         nc.sync.dma_start(out=xmean_b[:], in_=xmean.rearrange("(g p t) -> p g t", p=P, t=PACK))
         nc.vector.memset(as_rest[:].bitcast(I32), 0)
@@ -135,8 +135,8 @@ def tile_ensemble_kalman_residual_s4_kernel(
             nc.vector.tensor_copy(out=a_cod[sg][:].bitcast(U16), in_=raw_words(sg))
             nc.vector.tensor_copy(out=a_scl[sg][:], in_=raw_scales(sg))
 
-        def stage1(sg, h):
-            for t in range(PACK):
+        def stage1(sg, h, slots=range(PACK)):
+            for t in slots:
                 cod = a_cod0[t][:] if sg == 0 else a_cod[sg][:, t]
                 scl = a_scl0[t][:] if sg == 0 else a_scl[sg][:, t]
                 bank = next_bank()
@@ -158,9 +158,9 @@ def tile_ensemble_kalman_residual_s4_kernel(
                     scale=infl_f[:, sg, t : t + 1],
                 )
 
-        def interleave(sg, h, on_scalar=False):
-            dst = z_il[sg, h][:].rearrange("p (c j) t -> p c t j", j=4)
-            src = z_pl[sg, h][:].rearrange("p t (c j) -> p c t j", j=4)
+        def interleave(sg, h, on_scalar=False, lo=0, hi=NB):
+            dst = z_il[sg, h][:, lo:hi, :].rearrange("p (c j) t -> p c t j", j=4)
+            src = z_pl[sg, h][:, :, lo:hi].rearrange("p t (c j) -> p c t j", j=4)
             if on_scalar:
                 nc.scalar.copy(out=dst, in_=src)
             else:
@@ -203,8 +203,8 @@ def tile_ensemble_kalman_residual_s4_kernel(
                     start=(g == 0),
                     stop=(g == S_PASSES - 1),
                 )
-            diffs[k] = work.tile([P, NB], F32, name="diff", bufs=4)
-            results[k] = work.tile([P, NB], F32, name="res", bufs=6)
+            diffs[k] = work.tile([P, NB], F32, name="diff", bufs=4, align_bytes=SPAN)
+            results[k] = work.tile([P, NB], F32, name="res", bufs=6, align_bytes=SPAN)
             nc.vector.tensor_tensor(out=diffs[k][:, 0:w], in0=y_b[:, c0 : c0 + w], in1=bank[:, 0:w], op=ALU.subtract)
             multiply(k, nc.gpsimd, w - pool_columns(k), w)
 
@@ -254,7 +254,7 @@ def tile_ensemble_kalman_residual_s4_kernel(
         interleave(2, 1)
         stage1(3, 1)
         interleave(3, 1, on_scalar=True)
-        late = {0: 2, 5: 3}
+        late = {0: 2, 3: 3}
         for k in range(len(pieces)):
             stage2(k)
             if k > 0:

@@ -96,9 +96,9 @@ def tile_ensemble_kalman_residual_s4_kernel(
         nc.vector.memset(as_first[:].bitcast(I32), 0)
         nc.vector.memset(t_scl[:].bitcast(I32), 0)
         load_scale_rows(as_first, a_s[:, :, :, 0:128], [nc.sync, nc.scalar] * 2)
-        load_a(nc.sync, 0)
+        load_a(nc.scalar, 0)
         load_t(nc.scalar, 0)
-        load_scale_rows(t_scl, t_s, [nc.sync, nc.scalar] * 2)
+        load_scale_rows(t_scl, t_s, [nc.sync] * 4)
         nc.sync.dma_start(out=infl_b[:], in_=infl.rearrange("(g p t) -> p g t", p=P, t=PACK))
         nc.sync.dma_start(out=xmean_b[:], in_=xmean.rearrange("(g p t) -> p g t", p=P, t=PACK))
         nc.vector.memset(as_rest[:].bitcast(I32), 0)
@@ -222,7 +222,7 @@ def tile_ensemble_kalman_residual_s4_kernel(
             eng.dma_start(out=out[m * P : (m + 1) * P, c0 : c0 + w], in_=results[k][:, 0:w])
 
         idle = next_bank()
-        for rep in range(2):
+        for rep in range(3):
             nc.tensor.matmul_mx(
                 out=idle[:],
                 lhsT=as_first[:, 0, 0 : 2 * P].bitcast(FP4X4),

@@ -93,10 +93,10 @@ def tile_ensemble_kalman_residual_s4_kernel(
             for r in which:
                 queues[r].dma_start(out=plane[:].bitcast(I32)[r:P:32], in_=rows[r])
 
+        load_a(nc.scalar, 0)
         nc.vector.memset(as_first[:].bitcast(I32), 0)
         nc.vector.memset(t_scl[:].bitcast(I32), 0)
         load_scale_rows(as_first, a_s[:, :, :, 0:128], [nc.sync, nc.scalar] * 2)
-        load_a(nc.scalar, 0)
         load_t(nc.scalar, 0)
         load_scale_rows(t_scl, t_s, [nc.sync] * 4)
         nc.sync.dma_start(out=infl_b[:], in_=infl.rearrange("(g p t) -> p g t", p=P, t=PACK))

@@ -2,6 +2,7 @@ import math
 from contextlib import ExitStack
 
 import concourse.mybir as mybir
+from concourse.masks import make_identity
 
 E, S, OBS = 1024, 2048, 1024
 FLOPS = 2 * E * E * S + 2 * E * S * OBS
@@ -28,6 +29,8 @@ BANKS = 8
 WIDTH = {F32: 4, U32: 4, BF16: 2, U8: 1}
 SPAN = 256
 STATIONARY_SHIFT = 64
+TURNED_OBS = 2
+TURNED_MEMBERS = 2
 
 
 def tile_ensemble_kalman_residual_s4_kernel(
@@ -56,7 +59,8 @@ def tile_ensemble_kalman_residual_s4_kernel(
         a_scl = [None] + [kept("a_scl%d" % sg, [P, PACK, E_PASSES, P], U8, STATIONARY_SHIFT) for sg in range(1, S_PASSES)]
         t_cod = [kept("t_cod%d" % h, [P, E_PASSES, 2 * NB], U8) for h in range(HALVES)]
         t_scl = kept("t_scl", [P, E_PASSES, E], U8)
-        h_cod = [kept("h_cod%d" % g, [P, OBS], U32) for g in range(S_PASSES)]
+        h_pair = [kept("h_pair%d" % j, [P, 2, OBS], U32) for j in range(S_PASSES // 2)]
+        h_cod = [h_pair[g // 2][:, g % 2] for g in range(S_PASSES)]
         h_scl = kept("h_scl", [P, OBS], U8)
         infl_b = kept("infl_b", [P, S_PASSES, PACK], BF16)
         xmean_b = kept("xmean_b", [P, S_PASSES, PACK], BF16)
@@ -64,6 +68,13 @@ def tile_ensemble_kalman_residual_s4_kernel(
         xmean_f = kept("xmean_f", [P, S_PASSES, PACK], F32)
         y_b = kept("y_b", [P, OBS], BF16)
         rinv_b = kept("rinv_b", [P, OBS], BF16)
+        y_col = kept("y_col", [P, TURNED_OBS, 2], BF16)
+        rinv_col = kept("rinv_col", [P, TURNED_OBS, 2], BF16)
+        minus_rinv = kept("minus_rinv", [P, TURNED_OBS], F32)
+        y_rinv = kept("y_rinv", [P, TURNED_OBS], F32)
+        ident = kept("ident", [P, P], F32)
+        turned_res = [kept("turned_res%d" % u, [P, TURNED_MEMBERS * P], F32) for u in range(TURNED_OBS)]
+        turned_out = [kept("turned_out%d" % j, [P, TURNED_OBS * P], F32) for j in range(TURNED_MEMBERS)]
         steps = [(sg, h) for h in range(HALVES) for sg in range(S_PASSES)]
         z_pl = {s: kept("z_pl%d_%d" % s, [P, PACK, NB], BF16) for s in steps}
         z_il = {s: kept("z_il%d_%d" % s, [P, NB, PACK], BF16) for s in steps}
@@ -103,6 +114,8 @@ def tile_ensemble_kalman_residual_s4_kernel(
         nc.sync.dma_start(out=xmean_b[:], in_=xmean.rearrange("(g p t) -> p g t", p=P, t=PACK))
         nc.vector.memset(as_rest[:].bitcast(I32), 0)
         nc.vector.memset(h_scl[:].bitcast(I32), 0)
+        nc.vector.memset(ident[:], 0.0)
+        make_identity(nc, ident[:], nomemset=True)
         load_t(nc.sync, 1)
         load_a(nc.sync, 1)
         load_scale_rows(as_rest, a_s[:, :, :, 128:512], [nc.sync] * 4)
@@ -110,12 +123,17 @@ def tile_ensemble_kalman_residual_s4_kernel(
         load_a(nc.sync, 3)
         for q in range(4):
             nc.sync.dma_start(out=h_scl[:].bitcast(I32)[32 * q : 32 * q + 16, :], in_=h_s[:, 4 * q : 4 * q + 4, :])
-        for g in range(S_PASSES):
-            nc.sync.dma_start(
-                out=h_cod[g][:].bitcast(I32), in_=h_words[g].rearrange("p n t -> p (n t)").bitcast(I32)
-            )
+        h_w = h_words.rearrange("g p n t -> p g (n t)").bitcast(I32)
+        for j in range(S_PASSES // 2):
+            nc.sync.dma_start(out=h_pair[j][:].bitcast(I32), in_=h_w[:, 2 * j : 2 * j + 2, :])
         nc.sync.dma_start(out=y_b[:], in_=y.partition_broadcast(P))
         nc.sync.dma_start(out=rinv_b[:], in_=rinv.partition_broadcast(P))
+        turned_c0 = OBS - TURNED_OBS * P
+        with nc.allow_non_contiguous_dma(reason="one value of y and of rinv for each partition"):
+            for col, vec in ((y_col, y), (rinv_col, rinv)):
+                nc.sync.dma_start(
+                    out=col[:, :, 0:1], in_=vec[turned_c0:OBS].rearrange("(u p o) -> p u o", p=P, o=1)
+                )
 
         nc.scalar.activation(out=infl_f[:], in_=infl_b[:], func=ACT.Identity)
         nc.scalar.activation(out=xmean_f[:], in_=xmean_b[:], func=ACT.Identity)
@@ -173,21 +191,16 @@ def tile_ensemble_kalman_residual_s4_kernel(
                 in_=z_il[sg, h][:].rearrange("p n t -> p (n t)"),
             )
 
-        pieces = []
-        for m in range(E // P):
-            widths = [512, 512] if m < E // P - 1 else [512, 256, 256]
-            c0 = 0
-            for w in widths:
-                pieces.append((m, c0, w))
-                c0 += w
-        first_narrow = len(pieces) - 3
+        first_turned = E // P - TURNED_MEMBERS
+        wide = [(m, c0, NB) for m in range(E // P) for c0 in range(0, OBS, NB) if m < first_turned or c0 == 0]
+        narrow = [(m, NB, turned_c0 - NB) for m in range(first_turned, E // P)]
+        pieces = wide + narrow
 
         diffs = {}
         results = {}
 
-        def pool_columns(k):
-            m, c0, w = pieces[k]
-            return w if k % 2 == 1 and k < first_narrow else 0
+        def on_gpsimd(k):
+            return k % 2 == 1 and k < len(wide) - TURNED_MEMBERS
 
         def stage2(k):
             m, c0, w = pieces[k]
@@ -206,20 +219,51 @@ def tile_ensemble_kalman_residual_s4_kernel(
             diffs[k] = work.tile([P, NB], F32, name="diff", bufs=4, align_bytes=SPAN)
             results[k] = work.tile([P, NB], F32, name="res", bufs=6, align_bytes=SPAN)
             nc.vector.tensor_tensor(out=diffs[k][:, 0:w], in0=y_b[:, c0 : c0 + w], in1=bank[:, 0:w], op=ALU.subtract)
-            multiply(k, nc.gpsimd, w - pool_columns(k), w)
+            if on_gpsimd(k):
+                multiply(k, nc.gpsimd)
 
-        def multiply(k, eng, lo, hi):
+        def multiply(k, eng):
             m, c0, w = pieces[k]
-            if hi > lo:
-                eng.tensor_tensor(
-                    out=results[k][:, lo:hi], in0=diffs[k][:, lo:hi], in1=rinv_b[:, c0 + lo : c0 + hi], op=ALU.mult
-                )
+            eng.tensor_tensor(out=results[k][:, 0:w], in0=diffs[k][:, 0:w], in1=rinv_b[:, c0 : c0 + w], op=ALU.mult)
 
         def finish(k):
             m, c0, w = pieces[k]
-            multiply(k, nc.vector, 0, w - pool_columns(k))
-            eng = nc.scalar if k > first_narrow and (len(pieces) - k) % 2 == 1 else nc.sync
-            eng.dma_start(out=out[m * P : (m + 1) * P, c0 : c0 + w], in_=results[k][:, 0:w])
+            if not on_gpsimd(k):
+                multiply(k, nc.vector)
+            nc.sync.dma_start(out=out[m * P : (m + 1) * P, c0 : c0 + w], in_=results[k][:, 0:w])
+
+        def stage2_turned(u):
+            h, mc = divmod(first_turned * P, NB)
+            c0 = turned_c0 + u * P
+            w = TURNED_MEMBERS * P
+            bank = next_bank()
+            for g in range(S_PASSES):
+                nc.tensor.matmul_mx(
+                    out=bank[:, 0:w],
+                    lhsT=h_cod[g][:, c0 : c0 + P].bitcast(FP8X4),
+                    lhsT_scale=h_scl[4 * g : P, c0 : c0 + P],
+                    rhs=z_cod[g, h][:, mc : mc + w].bitcast(FP8X4),
+                    rhs_scale=z_scl[g, h][:, mc : mc + w],
+                    start=(g == 0),
+                    stop=(g == S_PASSES - 1),
+                )
+            nc.scalar.activation(
+                out=turned_res[u][:],
+                in_=bank[:, 0:w],
+                func=ACT.Identity,
+                bias=y_rinv[:, u : u + 1],
+                scale=minus_rinv[:, u : u + 1],
+            )
+
+        def turn_back(j):
+            bank = next_bank()
+            for u in range(TURNED_OBS):
+                nc.tensor.transpose(bank[:, u * P : (u + 1) * P], turned_res[u][:, j * P : (j + 1) * P], ident[:])
+            nc.scalar.copy(out=turned_out[j][:], in_=bank[:, 0 : TURNED_OBS * P])
+
+        def store_turned(j, eng):
+            m = first_turned + j
+            eng.dma_start(out=out[m * P : (m + 1) * P, turned_c0:OBS], in_=turned_out[j][:])
 
         idle = next_bank()
         for rep in range(3):
@@ -254,11 +298,23 @@ def tile_ensemble_kalman_residual_s4_kernel(
         interleave(2, 1)
         stage1(3, 1)
         interleave(3, 1, on_scalar=True)
+        nc.scalar.activation(out=minus_rinv[:], in_=rinv_col[:, :, 0], func=ACT.Identity, scale=-1.0)
+        nc.gpsimd.tensor_tensor(out=y_rinv[:], in0=y_col[:, :, 0], in1=rinv_col[:, :, 0], op=ALU.mult)
         late = {0: 2, 3: 3}
-        for k in range(len(pieces)):
+        for k in range(len(wide)):
             stage2(k)
             if k > 0:
                 finish(k - 1)
             if k in late:
                 quantize(late[k], 1)
+        for u in range(TURNED_OBS):
+            stage2_turned(u)
+            if u > 0:
+                finish(len(wide) - 1)
+                finish(len(wide))
+            stage2(len(wide) + u)
+        for j in range(TURNED_MEMBERS):
+            turn_back(j)
+        store_turned(0, nc.sync)
+        store_turned(1, nc.scalar)
         finish(len(pieces) - 1)

@@ -2,7 +2,6 @@ import math
 from contextlib import ExitStack
 
 import concourse.mybir as mybir
-from concourse.masks import make_identity
 
 E, S, OBS = 1024, 2048, 1024
 FLOPS = 2 * E * E * S + 2 * E * S * OBS
@@ -29,6 +28,7 @@ BANKS = 8
 WIDTH = {F32: 4, U32: 4, BF16: 2, U8: 1}
 SPAN = 256
 STATIONARY_SHIFT = 64
+WHOLE_ROW_TILES = 3
 TURNED_OBS = 2
 TURNED_MEMBERS = 2
 
@@ -52,16 +52,15 @@ def tile_ensemble_kalman_residual_s4_kernel(
 
         a_raw = [kept("a_raw%d" % sg, [P, E_PASSES, 2 * KP], U8) for sg in range(S_PASSES)]
         as_first = kept("as_first", [P, E_PASSES, KP], U8)
-        as_rest = kept("as_rest", [P, E_PASSES, S - KP], U8)
-        a_cod0 = [kept("a_cod0_%d" % t, [P, E_PASSES, 2 * P], U8, STATIONARY_SHIFT) for t in range(PACK)]
-        a_scl0 = [kept("a_scl0_%d" % t, [P, E_PASSES, P], U8, STATIONARY_SHIFT) for t in range(PACK)]
-        a_cod = [None] + [kept("a_cod%d" % sg, [P, PACK, E_PASSES, 2 * P], U8, STATIONARY_SHIFT) for sg in range(1, S_PASSES)]
-        a_scl = [None] + [kept("a_scl%d" % sg, [P, PACK, E_PASSES, P], U8, STATIONARY_SHIFT) for sg in range(1, S_PASSES)]
+        rest_bytes = E_PASSES * (S - KP)
+        zeroed_late = kept("zeroed_late", [P, rest_bytes + OBS], U8)
+        as_rest = zeroed_late[:, 0:rest_bytes].rearrange("p (g n) -> p g n", g=E_PASSES)
+        h_scl = zeroed_late[:, rest_bytes : rest_bytes + OBS]
+        a_cod = [kept("a_cod%d" % sg, [P, PACK, E_PASSES, 2 * P], U8, STATIONARY_SHIFT) for sg in range(S_PASSES)]
+        a_scl = [kept("a_scl%d" % sg, [P, PACK, E_PASSES, P], U8, STATIONARY_SHIFT) for sg in range(S_PASSES)]
         t_cod = [kept("t_cod%d" % h, [P, E_PASSES, 2 * NB], U8) for h in range(HALVES)]
         t_scl = kept("t_scl", [P, E_PASSES, E], U8)
-        h_pair = [kept("h_pair%d" % j, [P, 2, OBS], U32) for j in range(S_PASSES // 2)]
-        h_cod = [h_pair[g // 2][:, g % 2] for g in range(S_PASSES)]
-        h_scl = kept("h_scl", [P, OBS], U8)
+        h_cod = [kept("h_cod%d" % g, [P, OBS], U32) for g in range(S_PASSES)]
         infl_b = kept("infl_b", [P, S_PASSES, PACK], BF16)
         xmean_b = kept("xmean_b", [P, S_PASSES, PACK], BF16)
         infl_f = kept("infl_f", [P, S_PASSES, PACK], F32)
@@ -112,10 +111,16 @@ def tile_ensemble_kalman_residual_s4_kernel(
         load_scale_rows(t_scl, t_s, [nc.sync] * 4)
         nc.sync.dma_start(out=infl_b[:], in_=infl.rearrange("(g p t) -> p g t", p=P, t=PACK))
         nc.sync.dma_start(out=xmean_b[:], in_=xmean.rearrange("(g p t) -> p g t", p=P, t=PACK))
-        nc.vector.memset(as_rest[:].bitcast(I32), 0)
-        nc.vector.memset(h_scl[:].bitcast(I32), 0)
-        nc.vector.memset(ident[:], 0.0)
-        make_identity(nc, ident[:], nomemset=True)
+        nc.vector.memset(zeroed_late[:].bitcast(I32), 0)
+        nc.gpsimd.affine_select(
+            out=ident[:],
+            in_=h_scl[:, 0 : 4 * P].bitcast(F32),
+            pattern=[[-1, P]],
+            compare_op=ALU.not_equal,
+            fill=1.0,
+            base=0,
+            channel_multiplier=1,
+        )
         load_t(nc.sync, 1)
         load_a(nc.sync, 1)
         load_scale_rows(as_rest, a_s[:, :, :, 128:512], [nc.sync] * 4)
@@ -123,9 +128,10 @@ def tile_ensemble_kalman_residual_s4_kernel(
         load_a(nc.sync, 3)
         for q in range(4):
             nc.sync.dma_start(out=h_scl[:].bitcast(I32)[32 * q : 32 * q + 16, :], in_=h_s[:, 4 * q : 4 * q + 4, :])
-        h_w = h_words.rearrange("g p n t -> p g (n t)").bitcast(I32)
-        for j in range(S_PASSES // 2):
-            nc.sync.dma_start(out=h_pair[j][:].bitcast(I32), in_=h_w[:, 2 * j : 2 * j + 2, :])
+        for g in range(S_PASSES):
+            nc.sync.dma_start(
+                out=h_cod[g][:].bitcast(I32), in_=h_words[g].rearrange("p n t -> p (n t)").bitcast(I32)
+            )
         nc.sync.dma_start(out=y_b[:], in_=y.partition_broadcast(P))
         nc.sync.dma_start(out=rinv_b[:], in_=rinv.partition_broadcast(P))
         turned_c0 = OBS - TURNED_OBS * P
@@ -145,18 +151,15 @@ def tile_ensemble_kalman_residual_s4_kernel(
         def raw_words(sg):
             return a_raw[sg][:].bitcast(U16).rearrange("p g (m t) -> p t g m", t=PACK)
 
-        def deal_slot(t):
-            nc.vector.tensor_copy(out=a_cod0[t][:].bitcast(U16), in_=raw_words(0)[:, t])
-            nc.vector.tensor_copy(out=a_scl0[t][:], in_=raw_scales(0)[:, t])
-
-        def deal(sg):
+        def deal(sg, parts=1):
             nc.vector.tensor_copy(out=a_cod[sg][:].bitcast(U16), in_=raw_words(sg))
-            nc.vector.tensor_copy(out=a_scl[sg][:], in_=raw_scales(sg))
+            for t0 in range(0, PACK, PACK // parts):
+                slots = slice(t0, t0 + PACK // parts)
+                nc.vector.tensor_copy(out=a_scl[sg][:, slots], in_=raw_scales(sg)[:, slots])
 
         def stage1(sg, h, slots=range(PACK)):
             for t in slots:
-                cod = a_cod0[t][:] if sg == 0 else a_cod[sg][:, t]
-                scl = a_scl0[t][:] if sg == 0 else a_scl[sg][:, t]
+                cod, scl = a_cod[sg][:, t], a_scl[sg][:, t]
                 bank = next_bank()
                 for g in range(E_PASSES):
                     nc.tensor.matmul_mx(
@@ -197,6 +200,7 @@ def tile_ensemble_kalman_residual_s4_kernel(
         pieces = wide + narrow
 
         diffs = {}
+        rows = {}
         results = {}
 
         def on_gpsimd(k):
@@ -216,8 +220,10 @@ def tile_ensemble_kalman_residual_s4_kernel(
                     start=(g == 0),
                     stop=(g == S_PASSES - 1),
                 )
-            diffs[k] = work.tile([P, NB], F32, name="diff", bufs=4, align_bytes=SPAN)
-            results[k] = work.tile([P, NB], F32, name="res", bufs=6, align_bytes=SPAN)
+            diffs[k] = work.tile([P, NB], F32, name="diff", bufs=len(pieces), align_bytes=SPAN)
+            if c0 == 0:
+                rows[m] = work.tile([P, OBS], F32, name="res", bufs=E // P, align_bytes=SPAN)
+            results[k] = rows[m][:, c0 : c0 + w]
             nc.vector.tensor_tensor(out=diffs[k][:, 0:w], in0=y_b[:, c0 : c0 + w], in1=bank[:, 0:w], op=ALU.subtract)
             if on_gpsimd(k):
                 multiply(k, nc.gpsimd)
@@ -230,7 +236,10 @@ def tile_ensemble_kalman_residual_s4_kernel(
             m, c0, w = pieces[k]
             if not on_gpsimd(k):
                 multiply(k, nc.vector)
-            nc.sync.dma_start(out=out[m * P : (m + 1) * P, c0 : c0 + w], in_=results[k][:, 0:w])
+            if m >= WHOLE_ROW_TILES:
+                nc.sync.dma_start(out=out[m * P : (m + 1) * P, c0 : c0 + w], in_=results[k])
+            elif c0 > 0:
+                nc.sync.dma_start(out=out[m * P : (m + 1) * P, :], in_=rows[m][:])
 
         def stage2_turned(u):
             h, mc = divmod(first_turned * P, NB)
@@ -276,8 +285,7 @@ def tile_ensemble_kalman_residual_s4_kernel(
                 start=True,
                 stop=True,
             )
-        for t in range(PACK):
-            deal_slot(t)
+        deal(0, parts=2)
         stage1(0, 0)
         deal(1)
         stage1(0, 1)

@@ -29,6 +29,7 @@ WIDTH = {F32: 4, U32: 4, BF16: 2, U8: 1}
 SPAN = 256
 STATIONARY_SHIFT = 64
 WHOLE_ROW_TILES = 3
+LAST_QUANTIZE_BEHIND = 3
 TURNED_OBS = 2
 TURNED_MEMBERS = 2
 
@@ -74,11 +75,26 @@ def tile_ensemble_kalman_residual_s4_kernel(
         ident = kept("ident", [P, P], F32)
         turned_res = [kept("turned_res%d" % u, [P, TURNED_MEMBERS * P], F32) for u in range(TURNED_OBS)]
         turned_out = [kept("turned_out%d" % j, [P, TURNED_OBS * P], F32) for j in range(TURNED_MEMBERS)]
-        steps = [(sg, h) for h in range(HALVES) for sg in range(S_PASSES)]
-        z_pl = {s: kept("z_pl%d_%d" % s, [P, PACK, NB], BF16) for s in steps}
-        z_il = {s: kept("z_il%d_%d" % s, [P, NB, PACK], BF16) for s in steps}
-        z_cod = {s: kept("z_cod%d_%d" % s, [P, NB], U32, STATIONARY_SHIFT) for s in steps}
-        z_scl = {s: kept("z_scl%d_%d" % s, [P, NB], U8, STATIONARY_SHIFT) for s in steps}
+        copy_runs = [[(0, 0), (0, 1)], [(1, 0), (2, 0)], [(3, 0)], [(1, 1)], [(2, 1)], [(3, 1)]]
+        quantize_runs = copy_runs[:4] + [copy_runs[4] + copy_runs[5]]
+
+        def run_tiles(name, runs, shape, dtype, shift=0):
+            return [kept("%s%d" % (name, r), shape(len(run) * NB), dtype, shift) for r, run in enumerate(runs)]
+
+        def columns(runs, step):
+            r = [step in run for run in runs].index(True)
+            j = runs[r].index(step)
+            return r, slice(j * NB, (j + 1) * NB)
+
+        z_pl = run_tiles("z_pl", copy_runs, lambda n: [P, PACK, n], BF16)
+        z_il = run_tiles("z_il", quantize_runs, lambda n: [P, n, PACK], BF16)
+        z_cod_run = run_tiles("z_cod", quantize_runs, lambda n: [P, n], U32, STATIONARY_SHIFT)
+        z_scl_run = run_tiles("z_scl", quantize_runs, lambda n: [P, n], U8, STATIONARY_SHIFT)
+        z_cod, z_scl = {}, {}
+        for run in quantize_runs:
+            for step in run:
+                r, cols = columns(quantize_runs, step)
+                z_cod[step], z_scl[step] = z_cod_run[r][:, cols], z_scl_run[r][:, cols]
 
         banks_used = []
 
@@ -157,8 +173,9 @@ def tile_ensemble_kalman_residual_s4_kernel(
                 slots = slice(t0, t0 + PACK // parts)
                 nc.vector.tensor_copy(out=a_scl[sg][:, slots], in_=raw_scales(sg)[:, slots])
 
-        def stage1(sg, h, slots=range(PACK)):
-            for t in slots:
+        def stage1(sg, h):
+            r, cols = columns(copy_runs, (sg, h))
+            for t in range(PACK):
                 cod, scl = a_cod[sg][:, t], a_scl[sg][:, t]
                 bank = next_bank()
                 for g in range(E_PASSES):
@@ -172,26 +189,26 @@ def tile_ensemble_kalman_residual_s4_kernel(
                         stop=(g == E_PASSES - 1),
                     )
                 nc.scalar.activation(
-                    out=z_pl[sg, h][:, t, :],
+                    out=z_pl[r][:, t, cols],
                     in_=bank[:],
                     func=ACT.Identity,
                     bias=xmean_f[:, sg, t : t + 1],
                     scale=infl_f[:, sg, t : t + 1],
                 )
 
-        def interleave(sg, h, on_scalar=False, lo=0, hi=NB):
-            dst = z_il[sg, h][:, lo:hi, :].rearrange("p (c j) t -> p c t j", j=4)
-            src = z_pl[sg, h][:, :, lo:hi].rearrange("p t (c j) -> p c t j", j=4)
-            if on_scalar:
-                nc.scalar.copy(out=dst, in_=src)
-            else:
-                nc.vector.tensor_copy(out=dst, in_=src)
+        def interleave(r, copy):
+            rq, first = columns(quantize_runs, copy_runs[r][0])
+            cols = slice(first.start, first.start + len(copy_runs[r]) * NB)
+            copy(
+                out=z_il[rq][:, cols, :].rearrange("p (c j) t -> p c t j", j=4),
+                in_=z_pl[r][:].rearrange("p t (c j) -> p c t j", j=4),
+            )
 
-        def quantize(sg, h):
+        def quantize(r):
             nc.vector.quantize_mx(
-                out=z_cod[sg, h][:].bitcast(FP8X4),
-                scales=z_scl[sg, h][:],
-                in_=z_il[sg, h][:].rearrange("p n t -> p (n t)"),
+                out=z_cod_run[r][:].bitcast(FP8X4),
+                scales=z_scl_run[r][:],
+                in_=z_il[r][:].rearrange("p n t -> p (n t)"),
             )
 
         first_turned = E // P - TURNED_MEMBERS
@@ -287,34 +304,33 @@ def tile_ensemble_kalman_residual_s4_kernel(
             )
         deal(0, parts=2)
         stage1(0, 0)
-        deal(1)
+        for sg in range(1, S_PASSES):
+            deal(sg)
         stage1(0, 1)
-        deal(2)
-        interleave(0, 0)
-        deal(3)
-        quantize(0, 0)
-        interleave(0, 1)
-        for before, step in [((0, 1), (1, 0)), ((1, 0), (2, 0)), ((2, 0), (3, 0))]:
-            stage1(*step)
-            interleave(*step)
-            quantize(*before)
-        quantize(3, 0)
+        interleave(0, nc.vector.tensor_copy)
+        quantize(0)
+        stage1(1, 0)
+        stage1(2, 0)
+        interleave(1, nc.vector.tensor_copy)
+        stage1(3, 0)
+        interleave(2, nc.vector.tensor_copy)
+        quantize(1)
+        quantize(2)
         stage1(1, 1)
-        interleave(1, 1)
-        quantize(1, 1)
+        interleave(3, nc.vector.tensor_copy)
         stage1(2, 1)
-        interleave(2, 1)
+        interleave(4, nc.vector.tensor_copy)
+        quantize(3)
         stage1(3, 1)
-        interleave(3, 1, on_scalar=True)
+        interleave(5, nc.scalar.copy)
         nc.scalar.activation(out=minus_rinv[:], in_=rinv_col[:, :, 0], func=ACT.Identity, scale=-1.0)
         nc.gpsimd.tensor_tensor(out=y_rinv[:], in0=y_col[:, :, 0], in1=rinv_col[:, :, 0], op=ALU.mult)
-        late = {0: 2, 3: 3}
         for k in range(len(wide)):
             stage2(k)
             if k > 0:
                 finish(k - 1)
-            if k in late:
-                quantize(late[k], 1)
+            if k == LAST_QUANTIZE_BEHIND:
+                quantize(4)
         for u in range(TURNED_OBS):
             stage2_turned(u)
             if u > 0:

@@ -28,6 +28,7 @@ BANKS = 8
 WIDTH = {F32: 4, U32: 4, BF16: 2, U8: 1}
 SPAN = 256
 STATIONARY_SHIFT = 64
+WARM_UPS = 5
 WHOLE_ROW_TILES = 3
 LAST_QUANTIZE_BEHIND = 3
 TURNED_OBS = 2
@@ -53,10 +54,8 @@ def tile_ensemble_kalman_residual_s4_kernel(
 
         a_raw = [kept("a_raw%d" % sg, [P, E_PASSES, 2 * KP], U8) for sg in range(S_PASSES)]
         as_first = kept("as_first", [P, E_PASSES, KP], U8)
-        rest_bytes = E_PASSES * (S - KP)
-        zeroed_late = kept("zeroed_late", [P, rest_bytes + OBS], U8)
-        as_rest = zeroed_late[:, 0:rest_bytes].rearrange("p (g n) -> p g n", g=E_PASSES)
-        h_scl = zeroed_late[:, rest_bytes : rest_bytes + OBS]
+        as_rest = kept("as_rest", [P, E_PASSES, S - KP], U8)
+        h_scl = kept("h_scl", [P, OBS], U8)
         a_cod = [kept("a_cod%d" % sg, [P, PACK, E_PASSES, 2 * P], U8, STATIONARY_SHIFT) for sg in range(S_PASSES)]
         a_scl = [kept("a_scl%d" % sg, [P, PACK, E_PASSES, P], U8, STATIONARY_SHIFT) for sg in range(S_PASSES)]
         t_cod = [kept("t_cod%d" % h, [P, E_PASSES, 2 * NB], U8) for h in range(HALVES)]
@@ -96,6 +95,8 @@ def tile_ensemble_kalman_residual_s4_kernel(
                 r, cols = columns(quantize_runs, step)
                 z_cod[step], z_scl[step] = z_cod_run[r][:, cols], z_scl_run[r][:, cols]
 
+        t_stage = kept("t_stage", [P, E_PASSES, E], U8)
+
         banks_used = []
 
         def next_bank():
@@ -106,7 +107,7 @@ def tile_ensemble_kalman_residual_s4_kernel(
         a_w = a_words.bitcast(I32).rearrange("g p n -> p g n")
         t_w = t_words.bitcast(I32).rearrange("g p n -> p g n")
         a_s = a_scales.bitcast(I32).rearrange("g (q r) n -> r q g n", r=4)
-        t_s = t_scales.bitcast(I32).rearrange("g (q r) n -> r q g n", r=4)
+        t_s = t_scales.bitcast(I32).rearrange("g (q r) n -> q r g n", r=4)
         h_s = h_scales.bitcast(I32)
 
         def load_a(eng, sg):
@@ -119,15 +120,33 @@ def tile_ensemble_kalman_residual_s4_kernel(
             for r in which:
                 queues[r].dma_start(out=plane[:].bitcast(I32)[r:P:32], in_=rows[r])
 
+        def quadrant(plane, q):
+            return plane[:].bitcast(I32)[32 * q : 32 * q + 4]
+
+        nc.sync.dma_start(out=quadrant(t_stage, 0), in_=t_s[0])
+        nc.scalar.dma_start(out=quadrant(t_stage, 2), in_=t_s[2])
         load_a(nc.scalar, 0)
-        nc.vector.memset(as_first[:].bitcast(I32), 0)
-        nc.vector.memset(t_scl[:].bitcast(I32), 0)
-        load_scale_rows(as_first, a_s[:, :, :, 0:128], [nc.sync, nc.scalar] * 2)
+        for plane in (as_first, h_scl, t_scl, as_rest):
+            nc.vector.memset(plane[:].bitcast(I32), 0)
+        idle = next_bank()
+        for rep in range(WARM_UPS):
+            nc.tensor.matmul_mx(
+                out=idle[:],
+                lhsT=h_scl[:, 0 : 2 * P].bitcast(FP4X4),
+                lhsT_scale=h_scl[:, 0:P],
+                rhs=h_scl[:].bitcast(FP4X4),
+                rhs_scale=h_scl[:, 0:NB],
+                start=True,
+                stop=True,
+            )
+        load_scale_rows(as_first, a_s[:, :, :, 0:128], [nc.sync] * 3 + [nc.scalar])
         load_t(nc.scalar, 0)
-        load_scale_rows(t_scl, t_s, [nc.sync] * 4)
+        for q in (1, 3):
+            nc.sync.dma_start(out=quadrant(t_scl, q), in_=t_s[q])
+        for q in (0, 2):
+            nc.vector.tensor_copy(out=quadrant(t_scl, q), in_=quadrant(t_stage, q))
         nc.sync.dma_start(out=infl_b[:], in_=infl.rearrange("(g p t) -> p g t", p=P, t=PACK))
         nc.sync.dma_start(out=xmean_b[:], in_=xmean.rearrange("(g p t) -> p g t", p=P, t=PACK))
-        nc.vector.memset(zeroed_late[:].bitcast(I32), 0)
         nc.gpsimd.affine_select(
             out=ident[:],
             in_=h_scl[:, 0 : 4 * P].bitcast(F32),
@@ -291,17 +310,6 @@ def tile_ensemble_kalman_residual_s4_kernel(
             m = first_turned + j
             eng.dma_start(out=out[m * P : (m + 1) * P, turned_c0:OBS], in_=turned_out[j][:])
 
-        idle = next_bank()
-        for rep in range(3):
-            nc.tensor.matmul_mx(
-                out=idle[:],
-                lhsT=as_first[:, 0, 0 : 2 * P].bitcast(FP4X4),
-                lhsT_scale=as_first[:, 0, 0:P],
-                rhs=as_first[:].rearrange("p g n -> p (g n)").bitcast(FP4X4),
-                rhs_scale=as_first[:, 0, :],
-                start=True,
-                stop=True,
-            )
         deal(0, parts=2)
         stage1(0, 0)
         for sg in range(1, S_PASSES):

import math
from contextlib import ExitStack

import concourse.mybir as mybir

E, S, OBS = 1024, 2048, 1024
FLOPS = 2 * E * E * S + 2 * E * S * OBS

F32 = mybir.dt.float32
BF16 = mybir.dt.bfloat16
I32 = mybir.dt.int32
U32 = mybir.dt.uint32
U16 = mybir.dt.uint16
U8 = mybir.dt.uint8
FP4X4 = mybir.dt.float4_e2m1fn_x4
FP8X4 = mybir.dt.float8_e4m3fn_x4
ACT = mybir.ActivationFunctionType
ALU = mybir.AluOpType

P = 128
PACK = 4
KP = P * PACK
NB = 512
E_PASSES = E // KP
S_PASSES = S // KP
HALVES = E // NB
BANKS = 8
WIDTH = {F32: 4, U32: 4, BF16: 2, U8: 1}
SPAN = 256
STATIONARY_SHIFT = 64
WARM_UPS = 5
WHOLE_ROW_TILES = 3
LAST_QUANTIZE_BEHIND = 3
TURNED_OBS = 2
TURNED_MEMBERS = 2


def tile_ensemble_kalman_residual_s4_kernel(
    tc, a_words, a_scales, t_words, t_scales, h_words, h_scales, infl, xmean, y, rinv, out
):
    nc = tc.nc
    with ExitStack() as ctx:
        keep = ctx.enter_context(tc.tile_pool(name="keep", bufs=1))
        work = ctx.enter_context(tc.tile_pool(name="work", bufs=4))
        psum = ctx.enter_context(tc.psum_pool(name="psum", bufs=1))
        ctx.enter_context(tc.manual_schedule())

        ends = [0]

        def kept(name, shape, dtype, shift=0):
            start = (ends[-1] + SPAN - 1) // SPAN * SPAN + shift
            ends.append(start + math.prod(shape[1:]) * WIDTH[dtype])
            return keep.tile(shape, dtype, name=name, align_bytes=SPAN if start == 0 else 64, offset=start)

        a_raw = [kept("a_raw%d" % sg, [P, E_PASSES, 2 * KP], U8) for sg in range(S_PASSES)]
        as_first = kept("as_first", [P, E_PASSES, KP], U8)
        as_rest = kept("as_rest", [P, E_PASSES, S - KP], U8)
        h_scl = kept("h_scl", [P, OBS], U8)
        a_cod = [kept("a_cod%d" % sg, [P, PACK, E_PASSES, 2 * P], U8, STATIONARY_SHIFT) for sg in range(S_PASSES)]
        a_scl = [kept("a_scl%d" % sg, [P, PACK, E_PASSES, P], U8, STATIONARY_SHIFT) for sg in range(S_PASSES)]
        t_cod = [kept("t_cod%d" % h, [P, E_PASSES, 2 * NB], U8) for h in range(HALVES)]
        t_scl = kept("t_scl", [P, E_PASSES, E], U8)
        h_cod = [kept("h_cod%d" % g, [P, OBS], U32) for g in range(S_PASSES)]
        infl_b = kept("infl_b", [P, S_PASSES, PACK], BF16)
        xmean_b = kept("xmean_b", [P, S_PASSES, PACK], BF16)
        infl_f = kept("infl_f", [P, S_PASSES, PACK], F32)
        xmean_f = kept("xmean_f", [P, S_PASSES, PACK], F32)
        y_b = kept("y_b", [P, OBS], BF16)
        rinv_b = kept("rinv_b", [P, OBS], BF16)
        y_col = kept("y_col", [P, TURNED_OBS, 2], BF16)
        rinv_col = kept("rinv_col", [P, TURNED_OBS, 2], BF16)
        minus_rinv = kept("minus_rinv", [P, TURNED_OBS], F32)
        y_rinv = kept("y_rinv", [P, TURNED_OBS], F32)
        ident = kept("ident", [P, P], F32)
        turned_res = [kept("turned_res%d" % u, [P, TURNED_MEMBERS * P], F32) for u in range(TURNED_OBS)]
        turned_out = [kept("turned_out%d" % j, [P, TURNED_OBS * P], F32) for j in range(TURNED_MEMBERS)]
        copy_runs = [[(0, 0), (0, 1)], [(1, 0), (2, 0)], [(3, 0)], [(1, 1)], [(2, 1)], [(3, 1)]]
        quantize_runs = copy_runs[:4] + [copy_runs[4] + copy_runs[5]]

        def run_tiles(name, runs, shape, dtype, shift=0):
            return [kept("%s%d" % (name, r), shape(len(run) * NB), dtype, shift) for r, run in enumerate(runs)]

        def columns(runs, step):
            r = [step in run for run in runs].index(True)
            j = runs[r].index(step)
            return r, slice(j * NB, (j + 1) * NB)

        z_pl = run_tiles("z_pl", copy_runs, lambda n: [P, PACK, n], BF16)
        z_il = run_tiles("z_il", quantize_runs, lambda n: [P, n, PACK], BF16)
        z_cod_run = run_tiles("z_cod", quantize_runs, lambda n: [P, n], U32, STATIONARY_SHIFT)
        z_scl_run = run_tiles("z_scl", quantize_runs, lambda n: [P, n], U8, STATIONARY_SHIFT)
        z_cod, z_scl = {}, {}
        for run in quantize_runs:
            for step in run:
                r, cols = columns(quantize_runs, step)
                z_cod[step], z_scl[step] = z_cod_run[r][:, cols], z_scl_run[r][:, cols]

        t_stage = kept("t_stage", [P, E_PASSES, E], U8)

        banks_used = []

        def next_bank():
            b = len(banks_used) % BANKS
            banks_used.append(b)
            return psum.tile([P, NB], F32, name="bank%d" % b)

        a_w = a_words.bitcast(I32).rearrange("g p n -> p g n")
        t_w = t_words.bitcast(I32).rearrange("g p n -> p g n")
        a_s = a_scales.bitcast(I32).rearrange("g (q r) n -> r q g n", r=4)
        t_s = t_scales.bitcast(I32).rearrange("g (q r) n -> q r g n", r=4)
        h_s = h_scales.bitcast(I32)

        def load_a(eng, sg):
            eng.dma_start(out=a_raw[sg][:].bitcast(I32), in_=a_w[:, :, 256 * sg : 256 * (sg + 1)])

        def load_t(eng, h):
            eng.dma_start(out=t_cod[h][:].bitcast(I32), in_=t_w[:, :, 256 * h : 256 * (h + 1)])

        def load_scale_rows(plane, rows, queues, which=range(4)):
            for r in which:
                queues[r].dma_start(out=plane[:].bitcast(I32)[r:P:32], in_=rows[r])

        def quadrant(plane, q):
            return plane[:].bitcast(I32)[32 * q : 32 * q + 4]

        nc.sync.dma_start(out=quadrant(t_stage, 0), in_=t_s[0])
        nc.scalar.dma_start(out=quadrant(t_stage, 2), in_=t_s[2])
        load_a(nc.scalar, 0)
        for plane in (as_first, h_scl, t_scl, as_rest):
            nc.vector.memset(plane[:].bitcast(I32), 0)
        idle = next_bank()
        for rep in range(WARM_UPS):
            nc.tensor.matmul_mx(
                out=idle[:],
                lhsT=h_scl[:, 0 : 2 * P].bitcast(FP4X4),
                lhsT_scale=h_scl[:, 0:P],
                rhs=h_scl[:].bitcast(FP4X4),
                rhs_scale=h_scl[:, 0:NB],
                start=True,
                stop=True,
            )
        load_scale_rows(as_first, a_s[:, :, :, 0:128], [nc.sync] * 3 + [nc.scalar])
        load_t(nc.scalar, 0)
        for q in (1, 3):
            nc.sync.dma_start(out=quadrant(t_scl, q), in_=t_s[q])
        for q in (0, 2):
            nc.vector.tensor_copy(out=quadrant(t_scl, q), in_=quadrant(t_stage, q))
        nc.sync.dma_start(out=infl_b[:], in_=infl.rearrange("(g p t) -> p g t", p=P, t=PACK))
        nc.sync.dma_start(out=xmean_b[:], in_=xmean.rearrange("(g p t) -> p g t", p=P, t=PACK))
        nc.gpsimd.affine_select(
            out=ident[:],
            in_=h_scl[:, 0 : 4 * P].bitcast(F32),
            pattern=[[-1, P]],
            compare_op=ALU.not_equal,
            fill=1.0,
            base=0,
            channel_multiplier=1,
        )
        load_t(nc.sync, 1)
        load_a(nc.sync, 1)
        load_scale_rows(as_rest, a_s[:, :, :, 128:512], [nc.sync] * 4)
        load_a(nc.sync, 2)
        load_a(nc.sync, 3)
        for q in range(4):
            nc.sync.dma_start(out=h_scl[:].bitcast(I32)[32 * q : 32 * q + 16, :], in_=h_s[:, 4 * q : 4 * q + 4, :])
        for g in range(S_PASSES):
            nc.sync.dma_start(
                out=h_cod[g][:].bitcast(I32), in_=h_words[g].rearrange("p n t -> p (n t)").bitcast(I32)
            )
        nc.sync.dma_start(out=y_b[:], in_=y.partition_broadcast(P))
        nc.sync.dma_start(out=rinv_b[:], in_=rinv.partition_broadcast(P))
        turned_c0 = OBS - TURNED_OBS * P
        with nc.allow_non_contiguous_dma(reason="one value of y and of rinv for each partition"):
            for col, vec in ((y_col, y), (rinv_col, rinv)):
                nc.sync.dma_start(
                    out=col[:, :, 0:1], in_=vec[turned_c0:OBS].rearrange("(u p o) -> p u o", p=P, o=1)
                )

        nc.scalar.activation(out=infl_f[:], in_=infl_b[:], func=ACT.Identity)
        nc.scalar.activation(out=xmean_f[:], in_=xmean_b[:], func=ACT.Identity)

        def raw_scales(sg):
            raw = as_first[:] if sg == 0 else as_rest[:, :, KP * (sg - 1) : KP * sg]
            return raw.rearrange("p g (m t) -> p t g m", t=PACK)

        def raw_words(sg):
            return a_raw[sg][:].bitcast(U16).rearrange("p g (m t) -> p t g m", t=PACK)

        def deal(sg, parts=1):
            nc.vector.tensor_copy(out=a_cod[sg][:].bitcast(U16), in_=raw_words(sg))
            for t0 in range(0, PACK, PACK // parts):
                slots = slice(t0, t0 + PACK // parts)
                nc.vector.tensor_copy(out=a_scl[sg][:, slots], in_=raw_scales(sg)[:, slots])

        def stage1(sg, h):
            r, cols = columns(copy_runs, (sg, h))
            for t in range(PACK):
                cod, scl = a_cod[sg][:, t], a_scl[sg][:, t]
                bank = next_bank()
                for g in range(E_PASSES):
                    nc.tensor.matmul_mx(
                        out=bank[:],
                        lhsT=cod[:, g, :].bitcast(FP4X4),
                        lhsT_scale=scl[:, g, :],
                        rhs=t_cod[h][:, g, :].bitcast(FP4X4),
                        rhs_scale=t_scl[:, g, NB * h : NB * (h + 1)],
                        start=(g == 0),
                        stop=(g == E_PASSES - 1),
                    )
                nc.scalar.activation(
                    out=z_pl[r][:, t, cols],
                    in_=bank[:],
                    func=ACT.Identity,
                    bias=xmean_f[:, sg, t : t + 1],
                    scale=infl_f[:, sg, t : t + 1],
                )

        def interleave(r, copy):
            rq, first = columns(quantize_runs, copy_runs[r][0])
            cols = slice(first.start, first.start + len(copy_runs[r]) * NB)
            copy(
                out=z_il[rq][:, cols, :].rearrange("p (c j) t -> p c t j", j=4),
                in_=z_pl[r][:].rearrange("p t (c j) -> p c t j", j=4),
            )

        def quantize(r):
            nc.vector.quantize_mx(
                out=z_cod_run[r][:].bitcast(FP8X4),
                scales=z_scl_run[r][:],
                in_=z_il[r][:].rearrange("p n t -> p (n t)"),
            )

        first_turned = E // P - TURNED_MEMBERS
        wide = [(m, c0, NB) for m in range(E // P) for c0 in range(0, OBS, NB) if m < first_turned or c0 == 0]
        narrow = [(m, NB, turned_c0 - NB) for m in range(first_turned, E // P)]
        pieces = wide + narrow

        diffs = {}
        rows = {}
        results = {}

        def on_gpsimd(k):
            return k % 2 == 1 and k < len(wide) - TURNED_MEMBERS

        def stage2(k):
            m, c0, w = pieces[k]
            h, mc = divmod(m * P, NB)
            bank = next_bank()
            for g in range(S_PASSES):
                nc.tensor.matmul_mx(
                    out=bank[:, 0:w],
                    lhsT=z_cod[g, h][:, mc : mc + P].bitcast(FP8X4),
                    lhsT_scale=z_scl[g, h][:, mc : mc + P],
                    rhs=h_cod[g][:, c0 : c0 + w].bitcast(FP8X4),
                    rhs_scale=h_scl[4 * g : P, c0 : c0 + w],
                    start=(g == 0),
                    stop=(g == S_PASSES - 1),
                )
            diffs[k] = work.tile([P, NB], F32, name="diff", bufs=len(pieces), align_bytes=SPAN)
            if c0 == 0:
                rows[m] = work.tile([P, OBS], F32, name="res", bufs=E // P, align_bytes=SPAN)
            results[k] = rows[m][:, c0 : c0 + w]
            nc.vector.tensor_tensor(out=diffs[k][:, 0:w], in0=y_b[:, c0 : c0 + w], in1=bank[:, 0:w], op=ALU.subtract)
            if on_gpsimd(k):
                multiply(k, nc.gpsimd)

        def multiply(k, eng):
            m, c0, w = pieces[k]
            eng.tensor_tensor(out=results[k][:, 0:w], in0=diffs[k][:, 0:w], in1=rinv_b[:, c0 : c0 + w], op=ALU.mult)

        def finish(k):
            m, c0, w = pieces[k]
            if not on_gpsimd(k):
                multiply(k, nc.vector)
            if m >= WHOLE_ROW_TILES:
                nc.sync.dma_start(out=out[m * P : (m + 1) * P, c0 : c0 + w], in_=results[k])
            elif c0 > 0:
                nc.sync.dma_start(out=out[m * P : (m + 1) * P, :], in_=rows[m][:])

        def stage2_turned(u):
            h, mc = divmod(first_turned * P, NB)
            c0 = turned_c0 + u * P
            w = TURNED_MEMBERS * P
            bank = next_bank()
            for g in range(S_PASSES):
                nc.tensor.matmul_mx(
                    out=bank[:, 0:w],
                    lhsT=h_cod[g][:, c0 : c0 + P].bitcast(FP8X4),
                    lhsT_scale=h_scl[4 * g : P, c0 : c0 + P],
                    rhs=z_cod[g, h][:, mc : mc + w].bitcast(FP8X4),
                    rhs_scale=z_scl[g, h][:, mc : mc + w],
                    start=(g == 0),
                    stop=(g == S_PASSES - 1),
                )
            nc.scalar.activation(
                out=turned_res[u][:],
                in_=bank[:, 0:w],
                func=ACT.Identity,
                bias=y_rinv[:, u : u + 1],
                scale=minus_rinv[:, u : u + 1],
            )

        def turn_back(j):
            bank = next_bank()
            for u in range(TURNED_OBS):
                nc.tensor.transpose(bank[:, u * P : (u + 1) * P], turned_res[u][:, j * P : (j + 1) * P], ident[:])
            nc.scalar.copy(out=turned_out[j][:], in_=bank[:, 0 : TURNED_OBS * P])

        def store_turned(j, eng):
            m = first_turned + j
            eng.dma_start(out=out[m * P : (m + 1) * P, turned_c0:OBS], in_=turned_out[j][:])

        deal(0, parts=2)
        stage1(0, 0)
        for sg in range(1, S_PASSES):
            deal(sg)
        stage1(0, 1)
        interleave(0, nc.vector.tensor_copy)
        quantize(0)
        stage1(1, 0)
        stage1(2, 0)
        interleave(1, nc.vector.tensor_copy)
        stage1(3, 0)
        interleave(2, nc.vector.tensor_copy)
        quantize(1)
        quantize(2)
        stage1(1, 1)
        interleave(3, nc.vector.tensor_copy)
        stage1(2, 1)
        interleave(4, nc.vector.tensor_copy)
        quantize(3)
        stage1(3, 1)
        interleave(5, nc.scalar.copy)
        nc.scalar.activation(out=minus_rinv[:], in_=rinv_col[:, :, 0], func=ACT.Identity, scale=-1.0)
        nc.gpsimd.tensor_tensor(out=y_rinv[:], in0=y_col[:, :, 0], in1=rinv_col[:, :, 0], op=ALU.mult)
        for k in range(len(wide)):
            stage2(k)
            if k > 0:
                finish(k - 1)
            if k == LAST_QUANTIZE_BEHIND:
                quantize(4)
        for u in range(TURNED_OBS):
            stage2_turned(u)
            if u > 0:
                finish(len(wide) - 1)
                finish(len(wide))
            stage2(len(wide) + u)
        for j in range(TURNED_MEMBERS):
            turn_back(j)
        store_turned(0, nc.sync)
        store_turned(1, nc.scalar)
        finish(len(pieces) - 1)
